import numpy as np
import ml_dtypes


def mxq(x, axis, fmt="e4m3"):
    dtype, down = {"e4m3": (ml_dtypes.float8_e4m3fn, 7), "e5m2": (ml_dtypes.float8_e5m2, 14)}[fmt]
    v = np.moveaxis(np.asarray(x, np.float32).astype(ml_dtypes.bfloat16).astype(np.float64), axis, -1)
    blocks = v.reshape(v.shape[:-1] + (-1, 32))
    amax = np.abs(blocks).max(-1, keepdims=True)
    byte = np.maximum(np.where(amax > 0, np.frexp(amax)[1] - 1 + 127, 0) - down, 1)
    scale = np.exp2(byte - 127.0)
    codes = (blocks / scale).astype(np.float32).astype(dtype).astype(np.float64)
    return np.moveaxis((codes * scale).reshape(v.shape), -1, axis)


WIDE = False


def mx_kscale(k):
    if not WIDE:
        return np.ones(k)
    levels = np.array([10, -10, 5, -5, 0])
    if k % 512:
        return np.exp2(np.random.permutation(np.resize(levels, k // 32))).repeat(32)
    a = np.empty((k // 512, 16))
    for p in range(k // 512):
        a[p, :8] = np.random.permutation(np.resize(levels, 8))
        for g in range(8):
            far = levels[np.abs(levels - a[p, g]) >= 10]
            a[p, g + 8] = far[np.random.randint(len(far))]
    return np.exp2(a.ravel()).repeat(32)


def f64(x):
    return np.asarray(x).astype(np.float64)


def striped(idx):
    return np.tile(idx.reshape(-1, 16).T, (8, 1)).astype(np.uint16)


def unstriped(offs):
    return offs[:16].T.reshape(-1).astype(np.int64)


def sigmoid(v):
    return 1.0 / (1.0 + np.exp(-np.maximum(v, -700.0)))


K, T, S, N = 512, 2048, 512, 128


def setup_inputs():
    n = np.random.standard_normal
    s = mx_kscale(K)[:, None]
    return {
        "xT": (n((K, T)) * s).astype(np.float32),
        "w1": (n((K, N)) / np.sqrt(K) / s).astype(np.float32),
        "w2": (n((K, N)) / np.sqrt(K) / s).astype(np.float32),
        "w3": (n((K, N)) / np.sqrt(K) / s).astype(np.float32),
        "cell": n((N, T)).astype(np.float32),
        "offs": striped(np.random.permutation(T)[(T * np.random.uniform(0, 1, S) ** 4).astype(np.int64)]),
    }


def reference(xT, w1, w2, w3, cell, offs):
    xq = mxq(f64(xT)[:, unstriped(offs)], 0, "e4m3")
    f = sigmoid(mxq(f64(w1), 0, "e4m3").T @ xq)
    r = f64(cell)[:, unstriped(offs)]
    i = sigmoid(mxq(f64(w2), 0, "e4m3").T @ xq)
    g = np.tanh(mxq(f64(w3), 0, "e4m3").T @ xq)
    return f * r + i * g

@@ -1,0 +1,106 @@
+from contextlib import ExitStack
+
+import concourse.mybir as mybir
+
+K, T, S, N = 512, 2048, 512, 128
+FLOPS = 3 * 2 * K * N * S
+
+F32 = mybir.dt.float32
+BF16 = mybir.dt.bfloat16
+U32 = mybir.dt.uint32
+U16 = mybir.dt.uint16
+U8 = mybir.dt.uint8
+FP8X4 = mybir.dt.float8_e4m3fn_x4
+ACT = mybir.ActivationFunctionType
+ALU = mybir.AluOpType
+
+P = 128
+PACK = 4
+HALF = S // 2
+LANES = 16
+
+
+def tile_picked_beamcell_none_l_kernel(tc, xT, w1, w2, w3, cell, offs, out):
+    nc = tc.nc
+    with ExitStack() as ctx:
+        sb = ctx.enter_context(tc.tile_pool(name="sb", bufs=1))
+        ps = ctx.enter_context(tc.psum_pool(name="ps", bufs=1))
+
+        offsets = sb.tile([P, S // LANES], U16, name="offsets")
+        x_rows = [sb.tile([P, T], F32, name=f"x_rows{j}") for j in range(PACK)]
+        names = ("i", "g", "f")
+        weights = {"f": w1, "i": w2, "g": w3}
+        funcs = {"f": ACT.Sigmoid, "i": ACT.Sigmoid, "g": ACT.Tanh}
+        w_raw = {n: sb.tile([P, PACK, N], F32, name=f"w_raw_{n}") for n in names}
+        cell_rows = sb.tile([P, T], F32, name="cell_rows")
+
+        warm = sb.tile([P, 8], F32, name="warm")
+        warm_out = sb.tile([P, 8], F32, name="warm_out")
+        nc.gpsimd.memset(warm[:], 0.0)
+        nc.scalar.activation(warm_out[:], warm[:], ACT.Sigmoid)
+
+        x_planes = xT.rearrange("(p j) t -> p j t", j=PACK)
+        nc.sync.dma_start(x_rows[0][:], x_planes[:, 0, :])
+        nc.sync.dma_start(offsets[:], offs)
+        for j in range(1, PACK):
+            nc.sync.dma_start(x_rows[j][:], x_planes[:, j, :])
+        for n in names:
+            nc.sync.dma_start(w_raw[n][:], weights[n].rearrange("(p j) m -> p j m", j=PACK))
+        nc.sync.dma_start(cell_rows[:], cell)
+
+        cols = HALF // LANES
+        picks = [offsets[:, h * cols : (h + 1) * cols] for h in range(2)]
+
+        x_bf = [sb.tile([P, HALF, PACK], BF16, name=f"x_bf{h}", align_bytes=64) for h in range(2)]
+        for j in range(PACK):
+            for h in range(2):
+                nc.vector.tensor_copy(x_bf[h][:, :, j], x_rows[j][:].indirect(picks[h]))
+
+        w_codes, w_scales = {}, {}
+        w_bf = {}
+        for n in names:
+            w_bf[n] = sb.tile([P, N, PACK], BF16, name=f"w_bf_{n}", align_bytes=64)
+            nc.scalar.copy(w_bf[n][:], w_raw[n][:].rearrange("p j m -> p m j"))
+            w_codes[n] = sb.tile([P, N], U32, name=f"w_codes_{n}", align_bytes=64)
+            w_scales[n] = sb.tile([P, N], U8, name=f"w_scales_{n}", align_bytes=64)
+
+        def quantise_w(n):
+            nc.vector.quantize_mx(w_codes[n][:].bitcast(FP8X4), w_scales[n][:], w_bf[n][:].rearrange("p m j -> p (m j)"))
+
+        x_codes = [sb.tile([P, HALF], U32, name=f"x_codes{h}", align_bytes=64) for h in range(2)]
+        x_scales = [sb.tile([P, HALF], U8, name=f"x_scales{h}", align_bytes=64) for h in range(2)]
+
+        def quantise_x(h):
+            nc.vector.quantize_mx(x_codes[h][:].bitcast(FP8X4), x_scales[h][:], x_bf[h][:].rearrange("p s j -> p (s j)"))
+
+        quantise_w("i")
+        quantise_x(0)
+        quantise_w("g")
+        quantise_x(1)
+        quantise_w("f")
+
+        gate = {}
+        for h in range(2):
+            for n in names:
+                acc = ps.tile([P, HALF], F32, name=f"acc_{n}{h}")
+                nc.tensor.matmul_mx(
+                    acc[:],
+                    lhsT=w_codes[n][:].bitcast(FP8X4),
+                    lhsT_scale=w_scales[n][:],
+                    rhs=x_codes[h][:].bitcast(FP8X4),
+                    rhs_scale=x_scales[h][:],
+                    start=True,
+                    stop=True,
+                )
+                gate[n, h] = sb.tile([P, HALF], F32, name=f"gate_{n}{h}")
+                nc.scalar.activation(gate[n, h][:], acc[:], funcs[n])
+
+        fresh = [sb.tile([P, HALF], F32, name=f"fresh{h}") for h in range(2)]
+        kept = [sb.tile([P, HALF], F32, name=f"kept{h}") for h in range(2)]
+        result = [sb.tile([P, HALF], F32, name=f"result{h}") for h in range(2)]
+        for h in range(2):
+            nc.vector.tensor_tensor(fresh[h][:], gate["i", h][:], gate["g", h][:], ALU.mult)
+            nc.vector.tensor_tensor(kept[h][:], cell_rows[:].indirect(picks[h]), gate["f", h][:], ALU.mult)
+        for h in range(2):
+            nc.vector.tensor_tensor(result[h][:], kept[h][:], fresh[h][:], ALU.add)
+            nc.sync.dma_start(out[:, h * HALF : (h + 1) * HALF], result[h][:])

@@ -59,7 +59,7 @@ def tile_picked_beamcell_none_l_kernel(tc, xT, w1, w2, w3, cell, offs, out):
         w_codes, w_scales = {}, {}
         w_bf = {}
         for n in names:
-            w_bf[n] = sb.tile([P, N, PACK], BF16, name=f"w_bf_{n}", align_bytes=64)
+            w_bf[n] = sb.tile([P, N, PACK], BF16, name=f"w_bf_{n}", tag=f"w_bf_{n}", align_bytes=64)
             nc.scalar.copy(w_bf[n][:], w_raw[n][:].rearrange("p j m -> p m j"))
             w_codes[n] = sb.tile([P, N], U32, name=f"w_codes_{n}", align_bytes=64)
             w_scales[n] = sb.tile([P, N], U8, name=f"w_scales_{n}", align_bytes=64)
@@ -67,40 +67,48 @@ def tile_picked_beamcell_none_l_kernel(tc, xT, w1, w2, w3, cell, offs, out):
         def quantise_w(n):
             nc.vector.quantize_mx(w_codes[n][:].bitcast(FP8X4), w_scales[n][:], w_bf[n][:].rearrange("p m j -> p (m j)"))
 
-        x_codes = [sb.tile([P, HALF], U32, name=f"x_codes{h}", align_bytes=64) for h in range(2)]
+        x_codes = {}
         x_scales = [sb.tile([P, HALF], U8, name=f"x_scales{h}", align_bytes=64) for h in range(2)]
 
         def quantise_x(h):
+            x_codes[h] = sb.tile([P, HALF], U32, name=f"x_codes{h}", tag=("x_codes", "w_bf_f")[h], align_bytes=64)
             nc.vector.quantize_mx(x_codes[h][:].bitcast(FP8X4), x_scales[h][:], x_bf[h][:].rearrange("p s j -> p (s j)"))
 
         quantise_w("i")
         quantise_x(0)
         quantise_w("g")
-        quantise_x(1)
         quantise_w("f")
+        quantise_x(1)
 
         gate = {}
-        for h in range(2):
-            for n in names:
-                acc = ps.tile([P, HALF], F32, name=f"acc_{n}{h}")
-                nc.tensor.matmul_mx(
-                    acc[:],
-                    lhsT=w_codes[n][:].bitcast(FP8X4),
-                    lhsT_scale=w_scales[n][:],
-                    rhs=x_codes[h][:].bitcast(FP8X4),
-                    rhs_scale=x_scales[h][:],
-                    start=True,
-                    stop=True,
-                )
-                gate[n, h] = sb.tile([P, HALF], F32, name=f"gate_{n}{h}")
-                nc.scalar.activation(gate[n, h][:], acc[:], funcs[n])
+        for n, h in (("i", 0), ("g", 0), ("f", 0), ("f", 1), ("i", 1), ("g", 1)):
+            acc = ps.tile([P, HALF], F32, name=f"acc_{n}{h}")
+            nc.tensor.matmul_mx(
+                acc[:],
+                lhsT=w_codes[n][:].bitcast(FP8X4),
+                lhsT_scale=w_scales[n][:],
+                rhs=x_codes[h][:].bitcast(FP8X4),
+                rhs_scale=x_scales[h][:],
+                start=True,
+                stop=True,
+            )
+            gate[n, h] = sb.tile([P, HALF], F32, name=f"gate_{n}{h}")
+            nc.scalar.activation(gate[n, h][:], acc[:], funcs[n])
 
         fresh = [sb.tile([P, HALF], F32, name=f"fresh{h}") for h in range(2)]
         kept = [sb.tile([P, HALF], F32, name=f"kept{h}") for h in range(2)]
         result = [sb.tile([P, HALF], F32, name=f"result{h}") for h in range(2)]
-        for h in range(2):
+
+        def let_in(h):
             nc.vector.tensor_tensor(fresh[h][:], gate["i", h][:], gate["g", h][:], ALU.mult)
-            nc.vector.tensor_tensor(kept[h][:], cell_rows[:].indirect(picks[h]), gate["f", h][:], ALU.mult)
-        for h in range(2):
+
+        def finish(h):
             nc.vector.tensor_tensor(result[h][:], kept[h][:], fresh[h][:], ALU.add)
             nc.sync.dma_start(out[:, h * HALF : (h + 1) * HALF], result[h][:])
+
+        let_in(0)
+        for h in range(2):
+            nc.vector.tensor_tensor(kept[h][:], cell_rows[:].indirect(picks[h]), gate["f", h][:], ALU.mult)
+        let_in(1)
+        finish(0)
+        finish(1)

@@ -60,7 +60,10 @@ def tile_picked_beamcell_none_l_kernel(tc, xT, w1, w2, w3, cell, offs, out):
         w_bf = {}
         for n in names:
             w_bf[n] = sb.tile([P, N, PACK], BF16, name=f"w_bf_{n}", tag=f"w_bf_{n}", align_bytes=64)
-            nc.scalar.copy(w_bf[n][:], w_raw[n][:].rearrange("p j m -> p m j"))
+            nc.scalar.copy(
+                w_bf[n][:].rearrange("p (c e) j -> p c j e", e=4),
+                w_raw[n][:].rearrange("p j (c e) -> p c j e", e=4),
+            )
             w_codes[n] = sb.tile([P, N], U32, name=f"w_codes_{n}", align_bytes=64)
             w_scales[n] = sb.tile([P, N], U8, name=f"w_scales_{n}", align_bytes=64)
 

@@ -27,7 +27,8 @@ def tile_picked_beamcell_none_l_kernel(tc, xT, w1, w2, w3, cell, offs, out):
         ps = ctx.enter_context(tc.psum_pool(name="ps", bufs=1))
 
         offsets = sb.tile([P, S // LANES], U16, name="offsets")
-        x_rows = [sb.tile([P, T], F32, name=f"x_rows{j}") for j in range(PACK)]
+        x_first = sb.tile([P, 2, T], F32, name="x_first")
+        x_rows = {j: sb.tile([P, T], F32, name=f"x_rows{j}") for j in (2, 3)}
         names = ("i", "g", "f")
         weights = {"f": w1, "i": w2, "g": w3}
         funcs = {"f": ACT.Sigmoid, "i": ACT.Sigmoid, "g": ACT.Tanh}
@@ -40,9 +41,9 @@ def tile_picked_beamcell_none_l_kernel(tc, xT, w1, w2, w3, cell, offs, out):
         nc.scalar.activation(warm_out[:], warm[:], ACT.Sigmoid)
 
         x_planes = xT.rearrange("(p j) t -> p j t", j=PACK)
-        nc.sync.dma_start(x_rows[0][:], x_planes[:, 0, :])
+        nc.sync.dma_start(x_first[:], x_planes[:, 0:2, :])
         nc.sync.dma_start(offsets[:], offs)
-        for j in range(1, PACK):
+        for j in (2, 3):
             nc.sync.dma_start(x_rows[j][:], x_planes[:, j, :])
         for n in names:
             nc.sync.dma_start(w_raw[n][:], weights[n].rearrange("(p j) m -> p j m", j=PACK))
@@ -52,7 +53,12 @@ def tile_picked_beamcell_none_l_kernel(tc, xT, w1, w2, w3, cell, offs, out):
         picks = [offsets[:, h * cols : (h + 1) * cols] for h in range(2)]
 
         x_bf = [sb.tile([P, HALF, PACK], BF16, name=f"x_bf{h}", align_bytes=64) for h in range(2)]
-        for j in range(PACK):
+        for h in range(2):
+            picked = sb.tile([P, 2, HALF], F32, name=f"picked{h}")
+            for j in range(2):
+                nc.vector.tensor_copy(picked[:, j, :], x_first[:, j, :].indirect(picks[h]))
+            nc.scalar.copy(x_bf[h][:, :, 0:2], picked[:].rearrange("p j s -> p s j"))
+        for j in (2, 3):
             for h in range(2):
                 nc.vector.tensor_copy(x_bf[h][:, :, j], x_rows[j][:].indirect(picks[h]))
 

@@ -17,6 +17,7 @@ ALU = mybir.AluOpType
 P = 128
 PACK = 4
 HALF = S // 2
+QUARTER = S // 4
 LANES = 16
 
 
@@ -32,7 +33,7 @@ def tile_picked_beamcell_none_l_kernel(tc, xT, w1, w2, w3, cell, offs, out):
         names = ("i", "g", "f")
         weights = {"f": w1, "i": w2, "g": w3}
         funcs = {"f": ACT.Sigmoid, "i": ACT.Sigmoid, "g": ACT.Tanh}
-        w_raw = {n: sb.tile([P, PACK, N], F32, name=f"w_raw_{n}") for n in names}
+        w_raw = {n: sb.tile([P, PACK, N], F32, name=f"w_raw_{n}", tag=f"w_raw_{n}", align_bytes=64) for n in names}
         cell_rows = sb.tile([P, T], F32, name="cell_rows")
 
         warm = sb.tile([P, 8], F32, name="warm")
@@ -80,7 +81,7 @@ def tile_picked_beamcell_none_l_kernel(tc, xT, w1, w2, w3, cell, offs, out):
         x_scales = [sb.tile([P, HALF], U8, name=f"x_scales{h}", align_bytes=64) for h in range(2)]
 
         def quantise_x(h):
-            x_codes[h] = sb.tile([P, HALF], U32, name=f"x_codes{h}", tag=("x_codes", "w_bf_f")[h], align_bytes=64)
+            x_codes[h] = sb.tile([P, HALF], U32, name=f"x_codes{h}", tag=("x_codes", "w_raw_f")[h], align_bytes=64)
             nc.vector.quantize_mx(x_codes[h][:].bitcast(FP8X4), x_scales[h][:], x_bf[h][:].rearrange("p s j -> p (s j)"))
 
         quantise_w("i")
@@ -89,35 +90,57 @@ def tile_picked_beamcell_none_l_kernel(tc, xT, w1, w2, w3, cell, offs, out):
         quantise_w("f")
         quantise_x(1)
 
-        gate = {}
-        for n, h in (("i", 0), ("g", 0), ("f", 0), ("f", 1), ("i", 1), ("g", 1)):
-            acc = ps.tile([P, HALF], F32, name=f"acc_{n}{h}")
+        def make_gate(n, a, b):
+            h = a // HALF
+            cols_h = slice(a - h * HALF, b - h * HALF)
+            acc = ps.tile([P, b - a], F32, name=f"acc_{n}{a}")
             nc.tensor.matmul_mx(
                 acc[:],
                 lhsT=w_codes[n][:].bitcast(FP8X4),
                 lhsT_scale=w_scales[n][:],
-                rhs=x_codes[h][:].bitcast(FP8X4),
-                rhs_scale=x_scales[h][:],
+                rhs=x_codes[h][:, cols_h].bitcast(FP8X4),
+                rhs_scale=x_scales[h][:, cols_h],
                 start=True,
                 stop=True,
             )
-            gate[n, h] = sb.tile([P, HALF], F32, name=f"gate_{n}{h}")
-            nc.scalar.activation(gate[n, h][:], acc[:], funcs[n])
+            values = sb.tile([P, b - a], F32, name=f"gate_{n}{a}")
+            nc.scalar.activation(values[:], acc[:], funcs[n])
+            return values
+
+        i0 = make_gate("i", 0, HALF)
+        g0 = make_gate("g", 0, HALF)
+        f0 = [make_gate("f", u * QUARTER, (u + 1) * QUARTER) for u in range(2)]
+        f1 = make_gate("f", HALF, S)
+        i1 = make_gate("i", HALF, S)
+        g1 = make_gate("g", HALF, S)
 
         fresh = [sb.tile([P, HALF], F32, name=f"fresh{h}") for h in range(2)]
         kept = [sb.tile([P, HALF], F32, name=f"kept{h}") for h in range(2)]
         result = [sb.tile([P, HALF], F32, name=f"result{h}") for h in range(2)]
 
-        def let_in(h):
-            nc.vector.tensor_tensor(fresh[h][:], gate["i", h][:], gate["g", h][:], ALU.mult)
+        def keep(a, b, forget):
+            h = a // HALF
+            nc.vector.tensor_tensor(
+                kept[h][:, a - h * HALF : b - h * HALF],
+                cell_rows[:].indirect(offsets[:, a // LANES : b // LANES]),
+                forget,
+                ALU.mult,
+            )
 
-        def finish(h):
-            nc.vector.tensor_tensor(result[h][:], kept[h][:], fresh[h][:], ALU.add)
-            nc.sync.dma_start(out[:, h * HALF : (h + 1) * HALF], result[h][:])
+        def add(a, b):
+            h = a // HALF
+            c = slice(a - h * HALF, b - h * HALF)
+            nc.vector.tensor_tensor(result[h][:, c], kept[h][:, c], fresh[h][:, c], ALU.add)
 
-        let_in(0)
+        def store(a, b):
+            h = a // HALF
+            nc.sync.dma_start(out[:, a:b], result[h][:, a - h * HALF : b - h * HALF])
+
+        nc.vector.tensor_tensor(fresh[0][:], i0[:], g0[:], ALU.mult)
+        for u in range(2):
+            keep(u * QUARTER, (u + 1) * QUARTER, f0[u][:])
+        keep(HALF, S, f1[:])
+        nc.vector.tensor_tensor(fresh[1][:], i1[:], g1[:], ALU.mult)
         for h in range(2):
-            nc.vector.tensor_tensor(kept[h][:], cell_rows[:].indirect(picks[h]), gate["f", h][:], ALU.mult)
-        let_in(1)
-        finish(0)
-        finish(1)
+            add(h * HALF, (h + 1) * HALF)
+            store(h * HALF, (h + 1) * HALF)

@@ -80,20 +80,24 @@ def tile_picked_beamcell_none_l_kernel(tc, xT, w1, w2, w3, cell, offs, out):
         x_codes = {}
         x_scales = [sb.tile([P, HALF], U8, name=f"x_scales{h}", align_bytes=64) for h in range(2)]
 
-        def quantise_x(h):
-            x_codes[h] = sb.tile([P, HALF], U32, name=f"x_codes{h}", tag=("x_codes", "w_raw_f")[h], align_bytes=64)
-            nc.vector.quantize_mx(x_codes[h][:].bitcast(FP8X4), x_scales[h][:], x_bf[h][:].rearrange("p s j -> p (s j)"))
+        def quantise_x(h, a, b):
+            nc.vector.quantize_mx(
+                x_codes[h][:, a:b].bitcast(FP8X4), x_scales[h][:, a:b], x_bf[h][:, a:b, :].rearrange("p s j -> p (s j)")
+            )
 
         quantise_w("i")
-        quantise_x(0)
+        x_codes[0] = sb.tile([P, HALF], U32, name="x_codes0", tag="w_raw_i", align_bytes=64)
+        quantise_x(0, 0, QUARTER)
+        quantise_x(0, QUARTER, HALF)
         quantise_w("g")
+        x_codes[1] = sb.tile([P, HALF], U32, name="x_codes1", tag="w_raw_g", align_bytes=64)
+        quantise_x(1, 0, HALF)
         quantise_w("f")
-        quantise_x(1)
 
-        def make_gate(n, a, b):
+        def make_gate(n, a, b, values, bank):
             h = a // HALF
             cols_h = slice(a - h * HALF, b - h * HALF)
-            acc = ps.tile([P, b - a], F32, name=f"acc_{n}{a}")
+            acc = ps.tile([P, b - a], F32, name=f"acc_{n}{a}", tag=bank)
             nc.tensor.matmul_mx(
                 acc[:],
                 lhsT=w_codes[n][:].bitcast(FP8X4),
@@ -103,20 +107,30 @@ def tile_picked_beamcell_none_l_kernel(tc, xT, w1, w2, w3, cell, offs, out):
                 start=True,
                 stop=True,
             )
-            values = sb.tile([P, b - a], F32, name=f"gate_{n}{a}")
-            nc.scalar.activation(values[:], acc[:], funcs[n])
-            return values
+            nc.scalar.activation(values, acc[:], funcs[n])
 
-        i0 = make_gate("i", 0, HALF)
-        g0 = make_gate("g", 0, HALF)
-        f0 = [make_gate("f", u * QUARTER, (u + 1) * QUARTER) for u in range(2)]
-        f1 = make_gate("f", HALF, S)
-        i1 = make_gate("i", HALF, S)
-        g1 = make_gate("g", HALF, S)
-
+        q = [slice(u * QUARTER, (u + 1) * QUARTER) for u in range(2)]
+        i0 = sb.tile([P, HALF], F32, name="i0", tag="w_bf_g", align_bytes=64)
+        g0 = sb.tile([P, HALF], F32, name="g0")
+        i1 = sb.tile([P, HALF], F32, name="i1")
+        g1 = sb.tile([P, HALF], F32, name="g1")
+        f0a = sb.tile([P, QUARTER], F32, name="f0a")
+        f1 = sb.tile([P, HALF], F32, name="f1")
         fresh = [sb.tile([P, HALF], F32, name=f"fresh{h}") for h in range(2)]
+        f0b = fresh[1][:, q[1]]
         kept = [sb.tile([P, HALF], F32, name=f"kept{h}") for h in range(2)]
         result = [sb.tile([P, HALF], F32, name=f"result{h}") for h in range(2)]
+
+        make_gate("i", 0, QUARTER, i0[:, q[0]], "b0")
+        make_gate("i", QUARTER, HALF, i0[:, q[1]], "b1")
+        make_gate("g", 0, HALF, g0[:], "b2")
+        make_gate("i", HALF, HALF + QUARTER, i1[:, q[0]], "b3")
+        make_gate("g", HALF, HALF + QUARTER, g1[:, q[0]], "b4")
+        make_gate("f", 0, QUARTER, f0a[:], "b5")
+        make_gate("f", QUARTER, HALF, f0b, "b6")
+        make_gate("f", HALF, S, f1[:], "b7")
+        make_gate("i", HALF + QUARTER, S, i1[:, q[1]], "b5")
+        make_gate("g", HALF + QUARTER, S, g1[:, q[1]], "b6")
 
         def keep(a, b, forget):
             h = a // HALF
@@ -137,10 +151,11 @@ def tile_picked_beamcell_none_l_kernel(tc, xT, w1, w2, w3, cell, offs, out):
             nc.sync.dma_start(out[:, a:b], result[h][:, a - h * HALF : b - h * HALF])
 
         nc.vector.tensor_tensor(fresh[0][:], i0[:], g0[:], ALU.mult)
-        for u in range(2):
-            keep(u * QUARTER, (u + 1) * QUARTER, f0[u][:])
+        nc.vector.tensor_tensor(fresh[1][:, q[0]], i1[:, q[0]], g1[:, q[0]], ALU.mult)
+        keep(0, QUARTER, f0a[:])
+        keep(QUARTER, HALF, f0b)
         keep(HALF, S, f1[:])
-        nc.vector.tensor_tensor(fresh[1][:], i1[:], g1[:], ALU.mult)
+        nc.vector.tensor_tensor(fresh[1][:, q[1]], i1[:, q[1]], g1[:, q[1]], ALU.mult)
         for h in range(2):
             add(h * HALF, (h + 1) * HALF)
             store(h * HALF, (h + 1) * HALF)

@@ -109,53 +109,35 @@ def tile_picked_beamcell_none_l_kernel(tc, xT, w1, w2, w3, cell, offs, out):
             )
             nc.scalar.activation(values, acc[:], funcs[n])
 
-        q = [slice(u * QUARTER, (u + 1) * QUARTER) for u in range(2)]
         i0 = sb.tile([P, HALF], F32, name="i0", tag="w_bf_g", align_bytes=64)
         g0 = sb.tile([P, HALF], F32, name="g0")
         i1 = sb.tile([P, HALF], F32, name="i1")
         g1 = sb.tile([P, HALF], F32, name="g1")
-        f0a = sb.tile([P, QUARTER], F32, name="f0a")
-        f1 = sb.tile([P, HALF], F32, name="f1")
-        fresh = [sb.tile([P, HALF], F32, name=f"fresh{h}") for h in range(2)]
-        f0b = fresh[1][:, q[1]]
-        kept = [sb.tile([P, HALF], F32, name=f"kept{h}") for h in range(2)]
+        forget = sb.tile([P, S], F32, name="forget")
+        fresh0 = sb.tile([P, HALF], F32, name="fresh0")
+        kept = sb.tile([P, S], F32, name="kept")
         result = [sb.tile([P, HALF], F32, name=f"result{h}") for h in range(2)]
 
-        make_gate("i", 0, QUARTER, i0[:, q[0]], "b0")
-        make_gate("i", QUARTER, HALF, i0[:, q[1]], "b1")
+        make_gate("i", 0, QUARTER, i0[:, :QUARTER], "b0")
+        make_gate("i", QUARTER, HALF, i0[:, QUARTER:], "b1")
         make_gate("g", 0, HALF, g0[:], "b2")
-        make_gate("i", HALF, HALF + QUARTER, i1[:, q[0]], "b3")
-        make_gate("g", HALF, HALF + QUARTER, g1[:, q[0]], "b4")
-        make_gate("f", 0, QUARTER, f0a[:], "b5")
-        make_gate("f", QUARTER, HALF, f0b, "b6")
-        make_gate("f", HALF, S, f1[:], "b7")
-        make_gate("i", HALF + QUARTER, S, i1[:, q[1]], "b5")
-        make_gate("g", HALF + QUARTER, S, g1[:, q[1]], "b6")
+        make_gate("f", 0, QUARTER, forget[:, :QUARTER], "b3")
+        make_gate("f", QUARTER, HALF, forget[:, QUARTER:HALF], "b4")
+        make_gate("f", HALF, S, forget[:, HALF:], "b5")
+        make_gate("i", HALF, S, i1[:], "b2")
+        make_gate("g", HALF, S, g1[:], "b3")
 
-        def keep(a, b, forget):
-            h = a // HALF
+        def keep(a, b):
             nc.vector.tensor_tensor(
-                kept[h][:, a - h * HALF : b - h * HALF],
-                cell_rows[:].indirect(offsets[:, a // LANES : b // LANES]),
-                forget,
-                ALU.mult,
+                kept[:, a:b], cell_rows[:].indirect(offsets[:, a // LANES : b // LANES]), forget[:, a:b], ALU.mult
             )
 
-        def add(a, b):
-            h = a // HALF
-            c = slice(a - h * HALF, b - h * HALF)
-            nc.vector.tensor_tensor(result[h][:, c], kept[h][:, c], fresh[h][:, c], ALU.add)
-
-        def store(a, b):
-            h = a // HALF
-            nc.sync.dma_start(out[:, a:b], result[h][:, a - h * HALF : b - h * HALF])
-
-        nc.vector.tensor_tensor(fresh[0][:], i0[:], g0[:], ALU.mult)
-        nc.vector.tensor_tensor(fresh[1][:, q[0]], i1[:, q[0]], g1[:, q[0]], ALU.mult)
-        keep(0, QUARTER, f0a[:])
-        keep(QUARTER, HALF, f0b)
-        keep(HALF, S, f1[:])
-        nc.vector.tensor_tensor(fresh[1][:, q[1]], i1[:, q[1]], g1[:, q[1]], ALU.mult)
-        for h in range(2):
-            add(h * HALF, (h + 1) * HALF)
-            store(h * HALF, (h + 1) * HALF)
+        nc.vector.tensor_tensor(fresh0[:], i0[:], g0[:], ALU.mult)
+        keep(0, QUARTER)
+        keep(QUARTER, S)
+        fresh1 = sb.tile([P, HALF], F32, name="fresh1")
+        nc.vector.tensor_tensor(fresh1[:], i1[:], g1[:], ALU.mult)
+        for h, fresh in enumerate((fresh0, fresh1)):
+            cols_out = slice(h * HALF, (h + 1) * HALF)
+            nc.vector.tensor_tensor(result[h][:], kept[:, cols_out], fresh[:], ALU.add)
+            nc.sync.dma_start(out[:, cols_out], result[h][:])

@@ -18,6 +18,7 @@ P = 128
 PACK = 4
 HALF = S // 2
 QUARTER = S // 4
+EIGHTH = S // 8
 LANES = 16
 
 
@@ -54,11 +55,11 @@ def tile_picked_beamcell_none_l_kernel(tc, xT, w1, w2, w3, cell, offs, out):
         picks = [offsets[:, h * cols : (h + 1) * cols] for h in range(2)]
 
         x_bf = [sb.tile([P, HALF, PACK], BF16, name=f"x_bf{h}", align_bytes=64) for h in range(2)]
+        picked = sb.tile([P, 2, S], F32, name="picked")
+        for j in range(2):
+            nc.vector.tensor_copy(picked[:, j, :], x_first[:, j, :].indirect(offsets[:]))
         for h in range(2):
-            picked = sb.tile([P, 2, HALF], F32, name=f"picked{h}")
-            for j in range(2):
-                nc.vector.tensor_copy(picked[:, j, :], x_first[:, j, :].indirect(picks[h]))
-            nc.scalar.copy(x_bf[h][:, :, 0:2], picked[:].rearrange("p j s -> p s j"))
+            nc.scalar.copy(x_bf[h][:, :, 0:2], picked[:, :, h * HALF : (h + 1) * HALF].rearrange("p j s -> p s j"))
         for j in (2, 3):
             for h in range(2):
                 nc.vector.tensor_copy(x_bf[h][:, :, j], x_rows[j][:].indirect(picks[h]))
@@ -77,33 +78,32 @@ def tile_picked_beamcell_none_l_kernel(tc, xT, w1, w2, w3, cell, offs, out):
         def quantise_w(n):
             nc.vector.quantize_mx(w_codes[n][:].bitcast(FP8X4), w_scales[n][:], w_bf[n][:].rearrange("p m j -> p (m j)"))
 
-        x_codes = {}
-        x_scales = [sb.tile([P, HALF], U8, name=f"x_scales{h}", align_bytes=64) for h in range(2)]
+        x_scales = sb.tile([P, S], U8, name="x_scales", align_bytes=64)
 
-        def quantise_x(h, a, b):
+        def quantise_x(codes, a, b):
+            h = a // HALF
             nc.vector.quantize_mx(
-                x_codes[h][:, a:b].bitcast(FP8X4), x_scales[h][:, a:b], x_bf[h][:, a:b, :].rearrange("p s j -> p (s j)")
+                codes.bitcast(FP8X4), x_scales[:, a:b], x_bf[h][:, a - h * HALF : b - h * HALF, :].rearrange("p s j -> p (s j)")
             )
 
         quantise_w("i")
-        x_codes[0] = sb.tile([P, HALF], U32, name="x_codes0", tag="w_raw_i", align_bytes=64)
-        quantise_x(0, 0, QUARTER)
-        quantise_x(0, QUARTER, HALF)
+        codes_first = sb.tile([P, QUARTER], U32, name="codes_first", tag="w_raw_i", align_bytes=64)
+        quantise_x(codes_first[:], 0, QUARTER)
         quantise_w("g")
-        x_codes[1] = sb.tile([P, HALF], U32, name="x_codes1", tag="w_raw_g", align_bytes=64)
-        quantise_x(1, 0, HALF)
+        codes_rest = sb.tile([P, S - QUARTER], U32, name="codes_rest", tag="w_raw_g", align_bytes=64)
+        quantise_x(codes_rest[:, :QUARTER], QUARTER, HALF)
+        quantise_x(codes_rest[:, QUARTER:], HALF, S)
         quantise_w("f")
 
         def make_gate(n, a, b, values, bank):
-            h = a // HALF
-            cols_h = slice(a - h * HALF, b - h * HALF)
+            codes = codes_first[:, a:b] if a < QUARTER else codes_rest[:, a - QUARTER : b - QUARTER]
             acc = ps.tile([P, b - a], F32, name=f"acc_{n}{a}", tag=bank)
             nc.tensor.matmul_mx(
                 acc[:],
                 lhsT=w_codes[n][:].bitcast(FP8X4),
                 lhsT_scale=w_scales[n][:],
-                rhs=x_codes[h][:, cols_h].bitcast(FP8X4),
-                rhs_scale=x_scales[h][:, cols_h],
+                rhs=codes.bitcast(FP8X4),
+                rhs_scale=x_scales[:, a:b],
                 start=True,
                 stop=True,
             )
@@ -118,26 +118,29 @@ def tile_picked_beamcell_none_l_kernel(tc, xT, w1, w2, w3, cell, offs, out):
         kept = sb.tile([P, S], F32, name="kept")
         result = [sb.tile([P, HALF], F32, name=f"result{h}") for h in range(2)]
 
-        make_gate("i", 0, QUARTER, i0[:, :QUARTER], "b0")
-        make_gate("i", QUARTER, HALF, i0[:, QUARTER:], "b1")
-        make_gate("g", 0, HALF, g0[:], "b2")
-        make_gate("f", 0, QUARTER, forget[:, :QUARTER], "b3")
-        make_gate("f", QUARTER, HALF, forget[:, QUARTER:HALF], "b4")
-        make_gate("f", HALF, S, forget[:, HALF:], "b5")
-        make_gate("i", HALF, S, i1[:], "b2")
-        make_gate("g", HALF, S, g1[:], "b3")
+        for u in range(2):
+            c = slice(u * QUARTER, (u + 1) * QUARTER)
+            make_gate("i", c.start, c.stop, i0[:, c], f"b{2 * u}")
+            make_gate("g", c.start, c.stop, g0[:, c], f"b{2 * u + 1}")
+            nc.vector.tensor_tensor(fresh0[:, c], i0[:, c], g0[:, c], ALU.mult)
+        make_gate("f", 0, EIGHTH, forget[:, :EIGHTH], "b4")
+        make_gate("f", EIGHTH, QUARTER, forget[:, EIGHTH:QUARTER], "b5")
+        make_gate("f", QUARTER, HALF, forget[:, QUARTER:HALF], "b6")
+        make_gate("f", HALF, S, forget[:, HALF:], "b7")
+        make_gate("i", HALF, S, i1[:], "b3")
+        make_gate("g", HALF, S, g1[:], "b4")
 
         def keep(a, b):
             nc.vector.tensor_tensor(
                 kept[:, a:b], cell_rows[:].indirect(offsets[:, a // LANES : b // LANES]), forget[:, a:b], ALU.mult
             )
 
-        nc.vector.tensor_tensor(fresh0[:], i0[:], g0[:], ALU.mult)
-        keep(0, QUARTER)
-        keep(QUARTER, S)
-        fresh1 = sb.tile([P, HALF], F32, name="fresh1")
-        nc.vector.tensor_tensor(fresh1[:], i1[:], g1[:], ALU.mult)
-        for h, fresh in enumerate((fresh0, fresh1)):
+        keep(0, EIGHTH)
+        keep(EIGHTH, HALF)
+        keep(HALF, S)
+        fresh1 = forget[:, :HALF]
+        nc.vector.tensor_tensor(fresh1, i1[:], g1[:], ALU.mult)
+        for h, fresh in enumerate((fresh0[:], fresh1)):
             cols_out = slice(h * HALF, (h + 1) * HALF)
-            nc.vector.tensor_tensor(result[h][:], kept[:, cols_out], fresh[:], ALU.add)
+            nc.vector.tensor_tensor(result[h][:], kept[:, cols_out], fresh, ALU.add)
             nc.sync.dma_start(out[:, cols_out], result[h][:])

@@ -66,17 +66,22 @@ def tile_picked_beamcell_none_l_kernel(tc, xT, w1, w2, w3, cell, offs, out):
 
         w_codes, w_scales = {}, {}
         w_bf = {}
+        parts = {"i": [(0, N)], "g": [(0, N)], "f": [(0, N // 2), (N // 2, N)]}
         for n in names:
             w_bf[n] = sb.tile([P, N, PACK], BF16, name=f"w_bf_{n}", tag=f"w_bf_{n}", align_bytes=64)
-            nc.scalar.copy(
-                w_bf[n][:].rearrange("p (c e) j -> p c j e", e=4),
-                w_raw[n][:].rearrange("p j (c e) -> p c j e", e=4),
-            )
+            for a, b in parts[n]:
+                nc.scalar.copy(
+                    w_bf[n][:, a:b, :].rearrange("p (c e) j -> p c j e", e=4),
+                    w_raw[n][:, :, a:b].rearrange("p j (c e) -> p c j e", e=4),
+                )
             w_codes[n] = sb.tile([P, N], U32, name=f"w_codes_{n}", align_bytes=64)
             w_scales[n] = sb.tile([P, N], U8, name=f"w_scales_{n}", align_bytes=64)
 
         def quantise_w(n):
-            nc.vector.quantize_mx(w_codes[n][:].bitcast(FP8X4), w_scales[n][:], w_bf[n][:].rearrange("p m j -> p (m j)"))
+            for a, b in parts[n]:
+                nc.vector.quantize_mx(
+                    w_codes[n][:, a:b].bitcast(FP8X4), w_scales[n][:, a:b], w_bf[n][:, a:b, :].rearrange("p m j -> p (m j)")
+                )
 
         x_scales = sb.tile([P, S], U8, name="x_scales", align_bytes=64)
 
@@ -90,13 +95,14 @@ def tile_picked_beamcell_none_l_kernel(tc, xT, w1, w2, w3, cell, offs, out):
         codes_first = sb.tile([P, QUARTER], U32, name="codes_first", tag="w_raw_i", align_bytes=64)
         quantise_x(codes_first[:], 0, QUARTER)
         quantise_w("g")
-        codes_rest = sb.tile([P, S - QUARTER], U32, name="codes_rest", tag="w_raw_g", align_bytes=64)
-        quantise_x(codes_rest[:, :QUARTER], QUARTER, HALF)
-        quantise_x(codes_rest[:, QUARTER:], HALF, S)
+        codes_second = sb.tile([P, QUARTER], U32, name="codes_second", tag="w_raw_g", align_bytes=64)
+        quantise_x(codes_second[:], QUARTER, HALF)
         quantise_w("f")
+        codes_rest = sb.tile([P, HALF], U32, name="codes_rest", tag="w_raw_f", align_bytes=64)
+        quantise_x(codes_rest[:], HALF, S)
 
         def make_gate(n, a, b, values, bank):
-            codes = codes_first[:, a:b] if a < QUARTER else codes_rest[:, a - QUARTER : b - QUARTER]
+            codes = codes_first[:, a:b] if a < QUARTER else (codes_second[:] if a < HALF else codes_rest[:])
             acc = ps.tile([P, b - a], F32, name=f"acc_{n}{a}", tag=bank)
             nc.tensor.matmul_mx(
                 acc[:],

@@ -29,23 +29,23 @@ def tile_picked_beamcell_none_l_kernel(tc, xT, w1, w2, w3, cell, offs, out):
         ps = ctx.enter_context(tc.psum_pool(name="ps", bufs=1))
 
         offsets = sb.tile([P, S // LANES], U16, name="offsets")
-        x_first = sb.tile([P, 2, T], F32, name="x_first")
-        x_rows = {j: sb.tile([P, T], F32, name=f"x_rows{j}") for j in (2, 3)}
+        x_rows = {j: sb.tile([P, T], F32, name=f"x_rows{j}") for j in range(PACK)}
         names = ("i", "g", "f")
         weights = {"f": w1, "i": w2, "g": w3}
         funcs = {"f": ACT.Sigmoid, "i": ACT.Sigmoid, "g": ACT.Tanh}
         w_raw = {n: sb.tile([P, PACK, N], F32, name=f"w_raw_{n}", tag=f"w_raw_{n}", align_bytes=64) for n in names}
         cell_rows = sb.tile([P, T], F32, name="cell_rows")
 
+        x_planes = xT.rearrange("(p j) t -> p j t", j=PACK)
+        nc.scalar.dma_start(x_rows[0][:], x_planes[:, 0, :])
+
         warm = sb.tile([P, 8], F32, name="warm")
         warm_out = sb.tile([P, 8], F32, name="warm_out")
         nc.gpsimd.memset(warm[:], 0.0)
         nc.scalar.activation(warm_out[:], warm[:], ACT.Sigmoid)
 
-        x_planes = xT.rearrange("(p j) t -> p j t", j=PACK)
-        nc.sync.dma_start(x_first[:], x_planes[:, 0:2, :])
         nc.sync.dma_start(offsets[:], offs)
-        for j in (2, 3):
+        for j in (1, 2, 3):
             nc.sync.dma_start(x_rows[j][:], x_planes[:, j, :])
         for n in names:
             nc.sync.dma_start(w_raw[n][:], weights[n].rearrange("(p j) m -> p j m", j=PACK))
@@ -57,7 +57,7 @@ def tile_picked_beamcell_none_l_kernel(tc, xT, w1, w2, w3, cell, offs, out):
         x_bf = [sb.tile([P, HALF, PACK], BF16, name=f"x_bf{h}", align_bytes=64) for h in range(2)]
         picked = sb.tile([P, 2, S], F32, name="picked")
         for j in range(2):
-            nc.vector.tensor_copy(picked[:, j, :], x_first[:, j, :].indirect(offsets[:]))
+            nc.vector.tensor_copy(picked[:, j, :], x_rows[j][:].indirect(offsets[:]))
         for h in range(2):
             nc.scalar.copy(x_bf[h][:, :, 0:2], picked[:, :, h * HALF : (h + 1) * HALF].rearrange("p j s -> p s j"))
         for j in (2, 3):

@@ -29,7 +29,7 @@ def tile_picked_beamcell_none_l_kernel(tc, xT, w1, w2, w3, cell, offs, out):
         ps = ctx.enter_context(tc.psum_pool(name="ps", bufs=1))
 
         offsets = sb.tile([P, S // LANES], U16, name="offsets")
-        x_rows = {j: sb.tile([P, T], F32, name=f"x_rows{j}") for j in range(PACK)}
+        x_rows = {j: sb.tile([P, T], F32, name=f"x_rows{j}", tag=f"x_rows{j}", align_bytes=64) for j in range(PACK)}
         names = ("i", "g", "f")
         weights = {"f": w1, "i": w2, "g": w3}
         funcs = {"f": ACT.Sigmoid, "i": ACT.Sigmoid, "g": ACT.Tanh}
@@ -51,8 +51,8 @@ def tile_picked_beamcell_none_l_kernel(tc, xT, w1, w2, w3, cell, offs, out):
             nc.sync.dma_start(w_raw[n][:], weights[n].rearrange("(p j) m -> p j m", j=PACK))
         nc.sync.dma_start(cell_rows[:], cell)
 
-        cols = HALF // LANES
-        picks = [offsets[:, h * cols : (h + 1) * cols] for h in range(2)]
+        def picks(a, b):
+            return offsets[:, a // LANES : b // LANES]
 
         x_bf = [sb.tile([P, HALF, PACK], BF16, name=f"x_bf{h}", align_bytes=64) for h in range(2)]
         picked = sb.tile([P, 2, S], F32, name="picked")
@@ -60,15 +60,18 @@ def tile_picked_beamcell_none_l_kernel(tc, xT, w1, w2, w3, cell, offs, out):
             nc.vector.tensor_copy(picked[:, j, :], x_rows[j][:].indirect(offsets[:]))
         for h in range(2):
             nc.scalar.copy(x_bf[h][:, :, 0:2], picked[:, :, h * HALF : (h + 1) * HALF].rearrange("p j s -> p s j"))
-        for j in (2, 3):
-            for h in range(2):
-                nc.vector.tensor_copy(x_bf[h][:, :, j], x_rows[j][:].indirect(picks[h]))
+        for h in range(2):
+            nc.vector.tensor_copy(x_bf[h][:, :, 2], x_rows[2][:].indirect(picks(h * HALF, (h + 1) * HALF)))
 
-        w_codes, w_scales = {}, {}
-        w_bf = {}
+        last_plane = sb.tile([P, HALF], BF16, name="last_plane")
+        nc.scalar.activation(last_plane[:], x_rows[3][:].indirect(picks(HALF, S)), ACT.Copy)
+        nc.vector.tensor_copy(x_bf[0][:, :, 3], x_rows[3][:].indirect(picks(0, HALF)))
+        nc.vector.tensor_copy(x_bf[1][:, :, 3], last_plane[:])
+
+        w_codes, w_scales, w_bf = {}, {}, {}
         parts = {"i": [(0, N)], "g": [(0, N)], "f": [(0, N // 2), (N // 2, N)]}
         for n in names:
-            w_bf[n] = sb.tile([P, N, PACK], BF16, name=f"w_bf_{n}", tag=f"w_bf_{n}", align_bytes=64)
+            w_bf[n] = sb.tile([P, N, PACK], BF16, name=f"w_bf_{n}", align_bytes=64)
             for a, b in parts[n]:
                 nc.scalar.copy(
                     w_bf[n][:, a:b, :].rearrange("p (c e) j -> p c j e", e=4),
@@ -78,75 +81,78 @@ def tile_picked_beamcell_none_l_kernel(tc, xT, w1, w2, w3, cell, offs, out):
             w_scales[n] = sb.tile([P, N], U8, name=f"w_scales_{n}", align_bytes=64)
 
         def quantise_w(n):
-            for a, b in parts[n]:
-                nc.vector.quantize_mx(
-                    w_codes[n][:, a:b].bitcast(FP8X4), w_scales[n][:, a:b], w_bf[n][:, a:b, :].rearrange("p m j -> p (m j)")
-                )
+            nc.vector.quantize_mx(w_codes[n][:].bitcast(FP8X4), w_scales[n][:], w_bf[n][:].rearrange("p m j -> p (m j)"))
 
         x_scales = sb.tile([P, S], U8, name="x_scales", align_bytes=64)
+        codes_first = sb.tile([P, QUARTER], U32, name="codes_first", tag="x_rows3", align_bytes=64)
+        codes_rest = sb.tile([P, S - QUARTER], U32, name="codes_rest", tag="w_raw_i", align_bytes=64)
 
-        def quantise_x(codes, a, b):
+        def x_codes(a, b):
+            return codes_first[:, a:b] if a < QUARTER else codes_rest[:, a - QUARTER : b - QUARTER]
+
+        def quantise_x(a, b):
             h = a // HALF
             nc.vector.quantize_mx(
-                codes.bitcast(FP8X4), x_scales[:, a:b], x_bf[h][:, a - h * HALF : b - h * HALF, :].rearrange("p s j -> p (s j)")
+                x_codes(a, b).bitcast(FP8X4),
+                x_scales[:, a:b],
+                x_bf[h][:, a - h * HALF : b - h * HALF, :].rearrange("p s j -> p (s j)"),
             )
 
+        quantise_x(0, QUARTER)
         quantise_w("i")
-        codes_first = sb.tile([P, QUARTER], U32, name="codes_first", tag="w_raw_i", align_bytes=64)
-        quantise_x(codes_first[:], 0, QUARTER)
+        quantise_x(QUARTER, HALF)
+        quantise_x(HALF, S)
         quantise_w("g")
-        codes_second = sb.tile([P, QUARTER], U32, name="codes_second", tag="w_raw_g", align_bytes=64)
-        quantise_x(codes_second[:], QUARTER, HALF)
         quantise_w("f")
-        codes_rest = sb.tile([P, HALF], U32, name="codes_rest", tag="w_raw_f", align_bytes=64)
-        quantise_x(codes_rest[:], HALF, S)
 
         def make_gate(n, a, b, values, bank):
-            codes = codes_first[:, a:b] if a < QUARTER else (codes_second[:] if a < HALF else codes_rest[:])
-            acc = ps.tile([P, b - a], F32, name=f"acc_{n}{a}", tag=bank)
+            acc = ps.tile([P, b - a], F32, name=f"acc_{n}{a}", tag=f"bank{bank}")
             nc.tensor.matmul_mx(
                 acc[:],
                 lhsT=w_codes[n][:].bitcast(FP8X4),
                 lhsT_scale=w_scales[n][:],
-                rhs=codes.bitcast(FP8X4),
+                rhs=x_codes(a, b).bitcast(FP8X4),
                 rhs_scale=x_scales[:, a:b],
                 start=True,
                 stop=True,
             )
-            nc.scalar.activation(values, acc[:], funcs[n])
+            nc.scalar.activation(values, runs(acc[:]), funcs[n])
 
-        i0 = sb.tile([P, HALF], F32, name="i0", tag="w_bf_g", align_bytes=64)
-        g0 = sb.tile([P, HALF], F32, name="g0")
-        i1 = sb.tile([P, HALF], F32, name="i1")
-        g1 = sb.tile([P, HALF], F32, name="g1")
-        forget = sb.tile([P, S], F32, name="forget")
-        fresh0 = sb.tile([P, HALF], F32, name="fresh0")
+        def runs(ap):
+            return ap.rearrange("p (r c) -> p r c", c=EIGHTH)
+
+        i_first = w_raw["f"][:, :, : N // 2]
+        i_rest = sb.tile([P, HALF], F32, name="i_rest")
+        gate_g = sb.tile([P, S], F32, name="gate_g")
+        early = S - QUARTER
+        fresh_and_forget = sb.tile([P, early + S], F32, name="fresh_and_forget")
+        fresh = fresh_and_forget[:, :S]
+        forget = fresh_and_forget[:, early:]
         kept = sb.tile([P, S], F32, name="kept")
         result = [sb.tile([P, HALF], F32, name=f"result{h}") for h in range(2)]
 
-        for u in range(2):
-            c = slice(u * QUARTER, (u + 1) * QUARTER)
-            make_gate("i", c.start, c.stop, i0[:, c], f"b{2 * u}")
-            make_gate("g", c.start, c.stop, g0[:, c], f"b{2 * u + 1}")
-            nc.vector.tensor_tensor(fresh0[:, c], i0[:, c], g0[:, c], ALU.mult)
-        make_gate("f", 0, EIGHTH, forget[:, :EIGHTH], "b4")
-        make_gate("f", EIGHTH, QUARTER, forget[:, EIGHTH:QUARTER], "b5")
-        make_gate("f", QUARTER, HALF, forget[:, QUARTER:HALF], "b6")
-        make_gate("f", HALF, S, forget[:, HALF:], "b7")
-        make_gate("i", HALF, S, i1[:], "b3")
-        make_gate("g", HALF, S, g1[:], "b4")
+        make_gate("i", 0, QUARTER, i_first[:, 0:2, :], 0)
+        make_gate("i", QUARTER, HALF, i_first[:, 2:4, :], 1)
+        make_gate("i", HALF, early, runs(i_rest[:, :QUARTER]), 2)
+        for u in range(3):
+            make_gate("g", u * QUARTER, (u + 1) * QUARTER, runs(gate_g[:, u * QUARTER : (u + 1) * QUARTER]), 3 + u)
+        nc.vector.tensor_tensor(runs(fresh[:, :HALF]), i_first, runs(gate_g[:, :HALF]), ALU.mult)
+        nc.vector.tensor_tensor(fresh[:, HALF:early], i_rest[:, :QUARTER], gate_g[:, HALF:early], ALU.mult)
+        make_gate("f", 0, EIGHTH, runs(forget[:, :EIGHTH]), 6)
+        make_gate("f", EIGHTH, QUARTER, runs(forget[:, EIGHTH:QUARTER]), 7)
+        make_gate("f", QUARTER, HALF, runs(forget[:, QUARTER:HALF]), 0)
+        make_gate("f", HALF, S, runs(forget[:, HALF:]), 1)
+        make_gate("i", early, S, runs(i_rest[:, QUARTER:]), 6)
+        make_gate("g", early, S, runs(gate_g[:, early:]), 7)
 
         def keep(a, b):
-            nc.vector.tensor_tensor(
-                kept[:, a:b], cell_rows[:].indirect(offsets[:, a // LANES : b // LANES]), forget[:, a:b], ALU.mult
-            )
+            nc.vector.tensor_tensor(kept[:, a:b], cell_rows[:].indirect(picks(a, b)), forget[:, a:b], ALU.mult)
 
         keep(0, EIGHTH)
         keep(EIGHTH, HALF)
         keep(HALF, S)
-        fresh1 = forget[:, :HALF]
-        nc.vector.tensor_tensor(fresh1, i1[:], g1[:], ALU.mult)
-        for h, fresh in enumerate((fresh0[:], fresh1)):
-            cols_out = slice(h * HALF, (h + 1) * HALF)
-            nc.vector.tensor_tensor(result[h][:], kept[:, cols_out], fresh, ALU.add)
-            nc.sync.dma_start(out[:, cols_out], result[h][:])
+        nc.vector.tensor_tensor(fresh[:, early:], i_rest[:, QUARTER:], gate_g[:, early:], ALU.mult)
+        for h in range(2):
+            cols = slice(h * HALF, (h + 1) * HALF)
+            nc.vector.tensor_tensor(result[h][:], kept[:, cols], fresh[:, cols], ALU.add)
+            nc.sync.dma_start(out[:, cols], result[h][:])

@@ -105,10 +105,9 @@ def tile_picked_beamcell_none_l_kernel(tc, xT, w1, w2, w3, cell, offs, out):
         quantise_w("g")
         quantise_w("f")
 
-        def make_gate(n, a, b, values, bank):
-            acc = ps.tile([P, b - a], F32, name=f"acc_{n}{a}", tag=f"bank{bank}")
+        def product(acc, n, a, b):
             nc.tensor.matmul_mx(
-                acc[:],
+                acc,
                 lhsT=w_codes[n][:].bitcast(FP8X4),
                 lhsT_scale=w_scales[n][:],
                 rhs=x_codes(a, b).bitcast(FP8X4),
@@ -116,42 +115,50 @@ def tile_picked_beamcell_none_l_kernel(tc, xT, w1, w2, w3, cell, offs, out):
                 start=True,
                 stop=True,
             )
+
+        def make_gate(n, a, b, values, bank):
+            acc = ps.tile([P, b - a], F32, name=f"acc_{n}{a}", tag=f"bank{bank}")
+            product(acc[:], n, a, b)
             nc.scalar.activation(values, runs(acc[:]), funcs[n])
 
         def runs(ap):
             return ap.rearrange("p (r c) -> p r c", c=EIGHTH)
 
         i_first = w_raw["f"][:, :, : N // 2]
-        i_rest = sb.tile([P, HALF], F32, name="i_rest")
+        i_third = sb.tile([P, QUARTER], F32, name="i_third")
         gate_g = sb.tile([P, S], F32, name="gate_g")
         early = S - QUARTER
-        fresh_and_forget = sb.tile([P, early + S], F32, name="fresh_and_forget")
+        fresh_and_forget = sb.tile([P, early + S + QUARTER], F32, name="fresh_and_forget")
         fresh = fresh_and_forget[:, :S]
-        forget = fresh_and_forget[:, early:]
+        forget = fresh_and_forget[:, early : early + S]
+        i_last = fresh_and_forget[:, early + S :]
         kept = sb.tile([P, S], F32, name="kept")
         result = [sb.tile([P, HALF], F32, name=f"result{h}") for h in range(2)]
 
         make_gate("i", 0, QUARTER, i_first[:, 0:2, :], 0)
         make_gate("i", QUARTER, HALF, i_first[:, 2:4, :], 1)
-        make_gate("i", HALF, early, runs(i_rest[:, :QUARTER]), 2)
+        make_gate("i", HALF, early, runs(i_third[:]), 2)
         for u in range(3):
             make_gate("g", u * QUARTER, (u + 1) * QUARTER, runs(gate_g[:, u * QUARTER : (u + 1) * QUARTER]), 3 + u)
         nc.vector.tensor_tensor(runs(fresh[:, :HALF]), i_first, runs(gate_g[:, :HALF]), ALU.mult)
-        nc.vector.tensor_tensor(fresh[:, HALF:early], i_rest[:, :QUARTER], gate_g[:, HALF:early], ALU.mult)
-        make_gate("f", 0, EIGHTH, runs(forget[:, :EIGHTH]), 6)
-        make_gate("f", EIGHTH, QUARTER, runs(forget[:, EIGHTH:QUARTER]), 7)
-        make_gate("f", QUARTER, HALF, runs(forget[:, QUARTER:HALF]), 0)
-        make_gate("f", HALF, S, runs(forget[:, HALF:]), 1)
-        make_gate("i", early, S, runs(i_rest[:, QUARTER:]), 6)
-        make_gate("g", early, S, runs(gate_g[:, early:]), 7)
+        nc.vector.tensor_tensor(fresh[:, HALF:early], i_third[:], gate_g[:, HALF:early], ALU.mult)
+        make_gate("f", 0, QUARTER, runs(forget[:, :QUARTER]), 6)
+        make_gate("f", QUARTER, early, runs(forget[:, QUARTER:early]), 7)
+        acc_last = ps.tile([P, HALF], F32, name="acc_last", tag="bank0")
+        product(acc_last[:, :QUARTER], "f", early, S)
+        product(acc_last[:, QUARTER:], "i", early, S)
+        nc.scalar.activation(fresh_and_forget[:, 2 * early :], acc_last[:], ACT.Sigmoid)
+        make_gate("g", early, S, runs(gate_g[:, early:]), 5)
 
         def keep(a, b):
             nc.vector.tensor_tensor(kept[:, a:b], cell_rows[:].indirect(picks(a, b)), forget[:, a:b], ALU.mult)
 
-        keep(0, EIGHTH)
-        keep(EIGHTH, HALF)
-        keep(HALF, S)
-        nc.vector.tensor_tensor(fresh[:, early:], i_rest[:, QUARTER:], gate_g[:, early:], ALU.mult)
+        keep(0, QUARTER)
+        keep(QUARTER, early)
+        cell_last = sb.tile([P, QUARTER], F32, name="cell_last")
+        nc.scalar.activation(cell_last[:], cell_rows[:].indirect(picks(early, S)), ACT.Copy)
+        nc.vector.tensor_tensor(fresh[:, early:], i_last, gate_g[:, early:], ALU.mult)
+        nc.vector.tensor_tensor(kept[:, early:], cell_last[:], forget[:, early:], ALU.mult)
         for h in range(2):
             cols = slice(h * HALF, (h + 1) * HALF)
             nc.vector.tensor_tensor(result[h][:], kept[:, cols], fresh[:, cols], ALU.add)

@@ -69,7 +69,7 @@ def tile_picked_beamcell_none_l_kernel(tc, xT, w1, w2, w3, cell, offs, out):
         nc.vector.tensor_copy(x_bf[1][:, :, 3], last_plane[:])
 
         w_codes, w_scales, w_bf = {}, {}, {}
-        parts = {"i": [(0, N)], "g": [(0, N)], "f": [(0, N // 2), (N // 2, N)]}
+        parts = {"i": [(0, N // 2), (N // 2, N)], "g": [(0, N)], "f": [(0, N // 2), (N // 2, N)]}
         for n in names:
             w_bf[n] = sb.tile([P, N, PACK], BF16, name=f"w_bf_{n}", align_bytes=64)
             for a, b in parts[n]:
@@ -81,7 +81,10 @@ def tile_picked_beamcell_none_l_kernel(tc, xT, w1, w2, w3, cell, offs, out):
             w_scales[n] = sb.tile([P, N], U8, name=f"w_scales_{n}", align_bytes=64)
 
         def quantise_w(n):
-            nc.vector.quantize_mx(w_codes[n][:].bitcast(FP8X4), w_scales[n][:], w_bf[n][:].rearrange("p m j -> p (m j)"))
+            for a, b in parts[n]:
+                nc.vector.quantize_mx(
+                    w_codes[n][:, a:b].bitcast(FP8X4), w_scales[n][:, a:b], w_bf[n][:, a:b, :].rearrange("p m j -> p (m j)")
+                )
 
         x_scales = sb.tile([P, S], U8, name="x_scales", align_bytes=64)
         codes_first = sb.tile([P, QUARTER], U32, name="codes_first", tag="x_rows3", align_bytes=64)

@@ -56,8 +56,8 @@ def tile_picked_beamcell_none_l_kernel(tc, xT, w1, w2, w3, cell, offs, out):
 
         x_bf = [sb.tile([P, HALF, PACK], BF16, name=f"x_bf{h}", align_bytes=64) for h in range(2)]
         picked = sb.tile([P, 2, S], F32, name="picked")
-        for j in range(2):
-            nc.vector.tensor_copy(picked[:, j, :], x_rows[j][:].indirect(offsets[:]))
+        nc.scalar.activation(picked[:, 0, :], x_rows[0][:].indirect(offsets[:]), ACT.Copy)
+        nc.vector.tensor_copy(picked[:, 1, :], x_rows[1][:].indirect(offsets[:]))
         for h in range(2):
             nc.scalar.copy(x_bf[h][:, :, 0:2], picked[:, :, h * HALF : (h + 1) * HALF].rearrange("p j s -> p s j"))
         for h in range(2):

@@ -45,8 +45,9 @@ def tile_picked_beamcell_none_l_kernel(tc, xT, w1, w2, w3, cell, offs, out):
         nc.scalar.activation(warm_out[:], warm[:], ACT.Sigmoid)
 
         nc.sync.dma_start(offsets[:], offs)
-        for j in (1, 2, 3):
-            nc.sync.dma_start(x_rows[j][:], x_planes[:, j, :])
+        for j, step in ((1, 4), (2, 2), (3, 1)):
+            for first in range(step):
+                nc.sync.dma_start(x_rows[j][first:P:step, :], x_planes[first:P:step, j, :])
         for n in names:
             nc.sync.dma_start(w_raw[n][:], weights[n].rearrange("(p j) m -> p j m", j=PACK))
         nc.sync.dma_start(cell_rows[:], cell)

@@ -29,7 +29,8 @@ def tile_picked_beamcell_none_l_kernel(tc, xT, w1, w2, w3, cell, offs, out):
         ps = ctx.enter_context(tc.psum_pool(name="ps", bufs=1))
 
         offsets = sb.tile([P, S // LANES], U16, name="offsets")
-        x_rows = {j: sb.tile([P, T], F32, name=f"x_rows{j}", tag=f"x_rows{j}", align_bytes=64) for j in range(PACK)}
+        x_pair = sb.tile([P, 2 * T], F32, name="x_pair", align_bytes=64)
+        x_rows = {j: sb.tile([P, T], F32, name=f"x_rows{j}", tag=f"x_rows{j}", align_bytes=64) for j in (2, 3)}
         names = ("i", "g", "f")
         weights = {"f": w1, "i": w2, "g": w3}
         funcs = {"f": ACT.Sigmoid, "i": ACT.Sigmoid, "g": ACT.Tanh}
@@ -37,7 +38,8 @@ def tile_picked_beamcell_none_l_kernel(tc, xT, w1, w2, w3, cell, offs, out):
         cell_rows = sb.tile([P, T], F32, name="cell_rows")
 
         x_planes = xT.rearrange("(p j) t -> p j t", j=PACK)
-        nc.scalar.dma_start(x_rows[0][:], x_planes[:, 0, :])
+        pair_rows = x_planes[:, 0:2, :].rearrange("p j t -> p (j t)")
+        nc.scalar.dma_start(x_pair[0:P:4], pair_rows[0:P:4])
 
         warm = sb.tile([P, 8], F32, name="warm")
         warm_out = sb.tile([P, 8], F32, name="warm_out")
@@ -45,9 +47,11 @@ def tile_picked_beamcell_none_l_kernel(tc, xT, w1, w2, w3, cell, offs, out):
         nc.scalar.activation(warm_out[:], warm[:], ACT.Sigmoid)
 
         nc.sync.dma_start(offsets[:], offs)
-        for j, step in ((1, 4), (2, 2), (3, 1)):
-            for first in range(step):
-                nc.sync.dma_start(x_rows[j][first:P:step, :], x_planes[first:P:step, j, :])
+        for first in (1, 2, 3):
+            nc.sync.dma_start(x_pair[first:P:4], pair_rows[first:P:4])
+        for first, step in ((0, 4), (2, 4), (1, 2)):
+            nc.sync.dma_start(x_rows[2][first:P:step], x_planes[first:P:step, 2, :])
+        nc.sync.dma_start(x_rows[3][:], x_planes[:, 3, :])
         for n in names:
             nc.sync.dma_start(w_raw[n][:], weights[n].rearrange("(p j) m -> p j m", j=PACK))
         nc.sync.dma_start(cell_rows[:], cell)
@@ -57,8 +61,8 @@ def tile_picked_beamcell_none_l_kernel(tc, xT, w1, w2, w3, cell, offs, out):
 
         x_bf = [sb.tile([P, HALF, PACK], BF16, name=f"x_bf{h}", align_bytes=64) for h in range(2)]
         picked = sb.tile([P, 2, S], F32, name="picked")
-        nc.scalar.activation(picked[:, 0, :], x_rows[0][:].indirect(offsets[:]), ACT.Copy)
-        nc.vector.tensor_copy(picked[:, 1, :], x_rows[1][:].indirect(offsets[:]))
+        nc.scalar.activation(picked[:, 0, :], x_pair[:].indirect(offsets[:]), ACT.Copy)
+        nc.vector.tensor_copy(picked[:, 1, :], x_pair[:, T:].indirect(offsets[:]))
         for h in range(2):
             nc.scalar.copy(x_bf[h][:, :, 0:2], picked[:, :, h * HALF : (h + 1) * HALF].rearrange("p j s -> p s j"))
         for h in range(2):

@@ -39,7 +39,7 @@ def tile_picked_beamcell_none_l_kernel(tc, xT, w1, w2, w3, cell, offs, out):
 
         x_planes = xT.rearrange("(p j) t -> p j t", j=PACK)
         pair_rows = x_planes[:, 0:2, :].rearrange("p j t -> p (j t)")
-        nc.scalar.dma_start(x_pair[0:P:4], pair_rows[0:P:4])
+        nc.scalar.dma_start(x_pair[0:P:2], pair_rows[0:P:2])
 
         warm = sb.tile([P, 8], F32, name="warm")
         warm_out = sb.tile([P, 8], F32, name="warm_out")
@@ -47,11 +47,12 @@ def tile_picked_beamcell_none_l_kernel(tc, xT, w1, w2, w3, cell, offs, out):
         nc.scalar.activation(warm_out[:], warm[:], ACT.Sigmoid)
 
         nc.sync.dma_start(offsets[:], offs)
-        for first in (1, 2, 3):
+        for first in (1, 3):
             nc.sync.dma_start(x_pair[first:P:4], pair_rows[first:P:4])
         for first, step in ((0, 4), (2, 4), (1, 2)):
             nc.sync.dma_start(x_rows[2][first:P:step], x_planes[first:P:step, 2, :])
-        nc.sync.dma_start(x_rows[3][:], x_planes[:, 3, :])
+        for first in range(2):
+            nc.sync.dma_start(x_rows[3][first:P:2], x_planes[first:P:2, 3, :])
         for n in names:
             nc.sync.dma_start(w_raw[n][:], weights[n].rearrange("(p j) m -> p j m", j=PACK))
         nc.sync.dma_start(cell_rows[:], cell)

@@ -29,13 +29,13 @@ def tile_picked_beamcell_none_l_kernel(tc, xT, w1, w2, w3, cell, offs, out):
         ps = ctx.enter_context(tc.psum_pool(name="ps", bufs=1))
 
         offsets = sb.tile([P, S // LANES], U16, name="offsets")
-        x_pair = sb.tile([P, 2 * T], F32, name="x_pair", align_bytes=64)
-        x_rows = {j: sb.tile([P, T], F32, name=f"x_rows{j}", tag=f"x_rows{j}", align_bytes=64) for j in (2, 3)}
+        x_pair = sb.tile([P, 2 * T], F32, name="x_pair", align_bytes=256)
+        x_rows = {j: sb.tile([P, T], F32, name=f"x_rows{j}", tag=f"x_rows{j}", align_bytes=256) for j in (2, 3)}
         names = ("i", "g", "f")
         weights = {"f": w1, "i": w2, "g": w3}
         funcs = {"f": ACT.Sigmoid, "i": ACT.Sigmoid, "g": ACT.Tanh}
-        w_raw = {n: sb.tile([P, PACK, N], F32, name=f"w_raw_{n}", tag=f"w_raw_{n}", align_bytes=64) for n in names}
-        cell_rows = sb.tile([P, T], F32, name="cell_rows")
+        w_raw = {n: sb.tile([P, PACK, N], F32, name=f"w_raw_{n}", tag=f"w_raw_{n}", align_bytes=256) for n in names}
+        cell_rows = sb.tile([P, T], F32, name="cell_rows", align_bytes=256)
 
         x_planes = xT.rearrange("(p j) t -> p j t", j=PACK)
         pair_rows = x_planes[:, 0:2, :].rearrange("p j t -> p (j t)")
@@ -93,8 +93,8 @@ def tile_picked_beamcell_none_l_kernel(tc, xT, w1, w2, w3, cell, offs, out):
                 )
 
         x_scales = sb.tile([P, S], U8, name="x_scales", align_bytes=64)
-        codes_first = sb.tile([P, QUARTER], U32, name="codes_first", tag="x_rows3", align_bytes=64)
-        codes_rest = sb.tile([P, S - QUARTER], U32, name="codes_rest", tag="w_raw_i", align_bytes=64)
+        codes_first = sb.tile([P, QUARTER], U32, name="codes_first", tag="x_rows3", align_bytes=256)
+        codes_rest = sb.tile([P, S - QUARTER], U32, name="codes_rest", tag="w_raw_i", align_bytes=256)
 
         def x_codes(a, b):
             return codes_first[:, a:b] if a < QUARTER else codes_rest[:, a - QUARTER : b - QUARTER]
@@ -142,7 +142,7 @@ def tile_picked_beamcell_none_l_kernel(tc, xT, w1, w2, w3, cell, offs, out):
         forget = fresh_and_forget[:, early : early + S]
         i_last = fresh_and_forget[:, early + S :]
         kept = sb.tile([P, S], F32, name="kept")
-        result = [sb.tile([P, HALF], F32, name=f"result{h}") for h in range(2)]
+        result = [sb.tile([P, HALF], F32, name=f"result{h}", align_bytes=256) for h in range(2)]
 
         make_gate("i", 0, QUARTER, i_first[:, 0:2, :], 0)
         make_gate("i", QUARTER, HALF, i_first[:, 2:4, :], 1)

@@ -20,6 +20,9 @@ HALF = S // 2
 QUARTER = S // 4
 EIGHTH = S // 8
 LANES = 16
+EARLY = S - QUARTER
+I_SCALAR = 96
+CELL_VECTOR = S - 128
 
 
 def tile_picked_beamcell_none_l_kernel(tc, xT, w1, w2, w3, cell, offs, out):
@@ -60,59 +63,66 @@ def tile_picked_beamcell_none_l_kernel(tc, xT, w1, w2, w3, cell, offs, out):
         def picks(a, b):
             return offsets[:, a // LANES : b // LANES]
 
-        x_bf = [sb.tile([P, HALF, PACK], BF16, name=f"x_bf{h}", align_bytes=64) for h in range(2)]
+        def scalar_pick(values, window, a, b):
+            nc.scalar.activation(values, window.indirect(picks(a, b)), ACT.Copy)
+
+        x_bf = sb.tile([P, EARLY, PACK], BF16, name="x_bf", align_bytes=64)
         picked = sb.tile([P, 2, S], F32, name="picked")
-        nc.scalar.activation(picked[:, 0, :], x_pair[:].indirect(offsets[:]), ACT.Copy)
+        dense = sb.tile([P, PACK, HALF], BF16, name="dense")
+        late_planes = dense[:, :, QUARTER:]
+        scalar_pick(picked[:, 0, :], x_pair[:], 0, S)
         nc.vector.tensor_copy(picked[:, 1, :], x_pair[:, T:].indirect(offsets[:]))
-        for h in range(2):
-            nc.scalar.copy(x_bf[h][:, :, 0:2], picked[:, :, h * HALF : (h + 1) * HALF].rearrange("p j s -> p s j"))
-        for h in range(2):
-            nc.vector.tensor_copy(x_bf[h][:, :, 2], x_rows[2][:].indirect(picks(h * HALF, (h + 1) * HALF)))
+        for a, b in ((0, HALF), (HALF, EARLY)):
+            nc.scalar.copy(x_bf[:, a:b, 0:2], picked[:, :, a:b].rearrange("p j s -> p s j"))
+        nc.vector.tensor_copy(late_planes[:, 0:2, :], picked[:, :, EARLY:])
+        nc.vector.tensor_copy(x_bf[:, :, 2], x_rows[2][:].indirect(picks(0, EARLY)))
+        scalar_pick(late_planes[:, 2, :], x_rows[2][:], EARLY, S)
 
-        last_plane = sb.tile([P, HALF], BF16, name="last_plane")
-        nc.scalar.activation(last_plane[:], x_rows[3][:].indirect(picks(HALF, S)), ACT.Copy)
-        nc.vector.tensor_copy(x_bf[0][:, :, 3], x_rows[3][:].indirect(picks(0, HALF)))
-        nc.vector.tensor_copy(x_bf[1][:, :, 3], last_plane[:])
+        scalar_pick(dense[:, 3, :], x_rows[3][:], HALF, S)
+        nc.vector.tensor_copy(x_bf[:, :HALF, 3], x_rows[3][:].indirect(picks(0, HALF)))
+        nc.vector.tensor_copy(x_bf[:, HALF:, 3], dense[:, 3, :QUARTER])
 
-        w_codes, w_scales, w_bf = {}, {}, {}
-        parts = {"i": [(0, N // 2), (N // 2, N)], "g": [(0, N)], "f": [(0, N // 2), (N // 2, N)]}
-        for n in names:
-            w_bf[n] = sb.tile([P, N, PACK], BF16, name=f"w_bf_{n}", align_bytes=64)
-            for a, b in parts[n]:
-                nc.scalar.copy(
-                    w_bf[n][:, a:b, :].rearrange("p (c e) j -> p c j e", e=4),
-                    w_raw[n][:, :, a:b].rearrange("p j (c e) -> p c j e", e=4),
-                )
-            w_codes[n] = sb.tile([P, N], U32, name=f"w_codes_{n}", align_bytes=64)
-            w_scales[n] = sb.tile([P, N], U8, name=f"w_scales_{n}", align_bytes=64)
+        def interleave(copy, woven, planes):
+            copy(woven.rearrange("p (c e) j -> p c j e", e=4), planes.rearrange("p j (c e) -> p c j e", e=4))
 
-        def quantise_w(n):
-            for a, b in parts[n]:
-                nc.vector.quantize_mx(
-                    w_codes[n][:, a:b].bitcast(FP8X4), w_scales[n][:, a:b], w_bf[n][:, a:b, :].rearrange("p m j -> p (m j)")
-                )
+        w_bf = {n: sb.tile([P, N, PACK], BF16, name=f"w_bf_{n}", tag=f"w_bf_{n}", align_bytes=64) for n in names}
+        w_codes = {n: sb.tile([P, N], U32, name=f"w_codes_{n}", align_bytes=64) for n in names}
+        w_scales = {n: sb.tile([P, N], U8, name=f"w_scales_{n}", align_bytes=64) for n in names}
+        w_halves = [(0, N // 2), (N // 2, N)]
+        interleave(nc.scalar.copy, w_bf["i"][:, :I_SCALAR, :], w_raw["i"][:, :, :I_SCALAR])
+        interleave(nc.gpsimd.tensor_copy, w_bf["i"][:, I_SCALAR:, :], w_raw["i"][:, :, I_SCALAR:])
+        interleave(nc.scalar.copy, w_bf["g"][:], w_raw["g"][:])
+        for a, b in w_halves:
+            interleave(nc.scalar.copy, w_bf["f"][:, a:b, :], w_raw["f"][:, :, a:b])
+
+        def quantise(codes, scales, woven):
+            nc.vector.quantize_mx(codes.bitcast(FP8X4), scales, woven.rearrange("p c j -> p (c j)"))
+
+        def quantise_w(n, a, b):
+            quantise(w_codes[n][:, a:b], w_scales[n][:, a:b], w_bf[n][:, a:b, :])
 
         x_scales = sb.tile([P, S], U8, name="x_scales", align_bytes=64)
         codes_first = sb.tile([P, QUARTER], U32, name="codes_first", tag="x_rows3", align_bytes=256)
-        codes_rest = sb.tile([P, S - QUARTER], U32, name="codes_rest", tag="w_raw_i", align_bytes=256)
+        codes_mid = sb.tile([P, HALF], U32, name="codes_mid", tag="w_raw_i", align_bytes=256)
+        x_bf_late = sb.tile([P, QUARTER, PACK], BF16, name="x_bf_late", tag="w_raw_g", align_bytes=256)
+
+        quantise(codes_first[:], x_scales[:, :QUARTER], x_bf[:, :QUARTER, :])
+        quantise_w("i", 0, N)
+        for a in (QUARTER, HALF):
+            quantise(codes_mid[:, a - QUARTER : a], x_scales[:, a : a + QUARTER], x_bf[:, a : a + QUARTER, :])
+        quantise_w("g", 0, N)
+        interleave(nc.vector.tensor_copy, x_bf_late[:], late_planes)
+        for a, b in w_halves:
+            quantise_w("f", a, b)
+        codes_last = sb.tile([P, QUARTER], U32, name="codes_last", tag="w_bf_f", align_bytes=64)
+        quantise(codes_last[:], x_scales[:, EARLY:], x_bf_late[:])
 
         def x_codes(a, b):
-            return codes_first[:, a:b] if a < QUARTER else codes_rest[:, a - QUARTER : b - QUARTER]
-
-        def quantise_x(a, b):
-            h = a // HALF
-            nc.vector.quantize_mx(
-                x_codes(a, b).bitcast(FP8X4),
-                x_scales[:, a:b],
-                x_bf[h][:, a - h * HALF : b - h * HALF, :].rearrange("p s j -> p (s j)"),
-            )
-
-        quantise_x(0, QUARTER)
-        quantise_w("i")
-        quantise_x(QUARTER, HALF)
-        quantise_x(HALF, S)
-        quantise_w("g")
-        quantise_w("f")
+            if a < QUARTER:
+                return codes_first[:]
+            if a < EARLY:
+                return codes_mid[:, a - QUARTER : b - QUARTER]
+            return codes_last[:]
 
         def product(acc, n, a, b):
             nc.tensor.matmul_mx(
@@ -125,49 +135,45 @@ def tile_picked_beamcell_none_l_kernel(tc, xT, w1, w2, w3, cell, offs, out):
                 stop=True,
             )
 
+        def runs(ap):
+            return ap.rearrange("p (r c) -> p r c", c=EIGHTH)
+
         def make_gate(n, a, b, values, bank):
             acc = ps.tile([P, b - a], F32, name=f"acc_{n}{a}", tag=f"bank{bank}")
             product(acc[:], n, a, b)
             nc.scalar.activation(values, runs(acc[:]), funcs[n])
 
-        def runs(ap):
-            return ap.rearrange("p (r c) -> p r c", c=EIGHTH)
-
         i_first = w_raw["f"][:, :, : N // 2]
         i_third = sb.tile([P, QUARTER], F32, name="i_third")
         gate_g = sb.tile([P, S], F32, name="gate_g")
-        early = S - QUARTER
-        fresh_and_forget = sb.tile([P, early + S + QUARTER], F32, name="fresh_and_forget")
+        fresh_and_forget = sb.tile([P, EARLY + S + QUARTER], F32, name="fresh_and_forget")
         fresh = fresh_and_forget[:, :S]
-        forget = fresh_and_forget[:, early : early + S]
-        i_last = fresh_and_forget[:, early + S :]
+        forget = fresh_and_forget[:, EARLY : EARLY + S]
+        i_last = fresh_and_forget[:, EARLY + S :]
         kept = sb.tile([P, S], F32, name="kept")
         result = [sb.tile([P, HALF], F32, name=f"result{h}", align_bytes=256) for h in range(2)]
 
         make_gate("i", 0, QUARTER, i_first[:, 0:2, :], 0)
         make_gate("i", QUARTER, HALF, i_first[:, 2:4, :], 1)
-        make_gate("i", HALF, early, runs(i_third[:]), 2)
+        make_gate("i", HALF, EARLY, runs(i_third[:]), 2)
         for u in range(3):
             make_gate("g", u * QUARTER, (u + 1) * QUARTER, runs(gate_g[:, u * QUARTER : (u + 1) * QUARTER]), 3 + u)
         nc.vector.tensor_tensor(runs(fresh[:, :HALF]), i_first, runs(gate_g[:, :HALF]), ALU.mult)
-        nc.vector.tensor_tensor(fresh[:, HALF:early], i_third[:], gate_g[:, HALF:early], ALU.mult)
+        nc.vector.tensor_tensor(fresh[:, HALF:EARLY], i_third[:], gate_g[:, HALF:EARLY], ALU.mult)
         make_gate("f", 0, QUARTER, runs(forget[:, :QUARTER]), 6)
-        make_gate("f", QUARTER, early, runs(forget[:, QUARTER:early]), 7)
+        make_gate("f", QUARTER, EARLY, runs(forget[:, QUARTER:EARLY]), 7)
         acc_last = ps.tile([P, HALF], F32, name="acc_last", tag="bank0")
-        product(acc_last[:, :QUARTER], "f", early, S)
-        product(acc_last[:, QUARTER:], "i", early, S)
-        nc.scalar.activation(fresh_and_forget[:, 2 * early :], acc_last[:], ACT.Sigmoid)
-        make_gate("g", early, S, runs(gate_g[:, early:]), 5)
+        product(acc_last[:, :QUARTER], "f", EARLY, S)
+        product(acc_last[:, QUARTER:], "i", EARLY, S)
+        nc.scalar.activation(fresh_and_forget[:, 2 * EARLY :], acc_last[:], ACT.Sigmoid)
+        make_gate("g", EARLY, S, runs(gate_g[:, EARLY:]), 5)
 
-        def keep(a, b):
+        for a, b in ((0, QUARTER), (QUARTER, CELL_VECTOR)):
             nc.vector.tensor_tensor(kept[:, a:b], cell_rows[:].indirect(picks(a, b)), forget[:, a:b], ALU.mult)
-
-        keep(0, QUARTER)
-        keep(QUARTER, early)
-        cell_last = sb.tile([P, QUARTER], F32, name="cell_last")
-        nc.scalar.activation(cell_last[:], cell_rows[:].indirect(picks(early, S)), ACT.Copy)
-        nc.vector.tensor_tensor(fresh[:, early:], i_last, gate_g[:, early:], ALU.mult)
-        nc.vector.tensor_tensor(kept[:, early:], cell_last[:], forget[:, early:], ALU.mult)
+        cell_last = sb.tile([P, S - CELL_VECTOR], F32, name="cell_last")
+        nc.scalar.activation(cell_last[:], cell_rows[:].indirect(picks(CELL_VECTOR, S)), ACT.Copy)
+        nc.vector.tensor_tensor(fresh[:, EARLY:], i_last, gate_g[:, EARLY:], ALU.mult)
+        nc.vector.tensor_tensor(kept[:, CELL_VECTOR:], cell_last[:], forget[:, CELL_VECTOR:], ALU.mult)
         for h in range(2):
             cols = slice(h * HALF, (h + 1) * HALF)
             nc.vector.tensor_tensor(result[h][:], kept[:, cols], fresh[:, cols], ALU.add)

@@ -85,12 +85,15 @@ def tile_picked_beamcell_none_l_kernel(tc, xT, w1, w2, w3, cell, offs, out):
         def interleave(copy, woven, planes):
             copy(woven.rearrange("p (c e) j -> p c j e", e=4), planes.rearrange("p j (c e) -> p c j e", e=4))
 
+        def gpsimd_round(rounded, values):
+            nc.gpsimd.tensor_scalar(rounded, values, 1.0, 0.0, ALU.mult, ALU.add)
+
         w_bf = {n: sb.tile([P, N, PACK], BF16, name=f"w_bf_{n}", tag=f"w_bf_{n}", align_bytes=64) for n in names}
         w_codes = {n: sb.tile([P, N], U32, name=f"w_codes_{n}", align_bytes=64) for n in names}
         w_scales = {n: sb.tile([P, N], U8, name=f"w_scales_{n}", align_bytes=64) for n in names}
         w_halves = [(0, N // 2), (N // 2, N)]
         interleave(nc.scalar.copy, w_bf["i"][:, :I_SCALAR, :], w_raw["i"][:, :, :I_SCALAR])
-        interleave(nc.gpsimd.tensor_copy, w_bf["i"][:, I_SCALAR:, :], w_raw["i"][:, :, I_SCALAR:])
+        interleave(gpsimd_round, w_bf["i"][:, I_SCALAR:, :], w_raw["i"][:, :, I_SCALAR:])
         interleave(nc.scalar.copy, w_bf["g"][:], w_raw["g"][:])
         for a, b in w_halves:
             interleave(nc.scalar.copy, w_bf["f"][:, a:b, :], w_raw["f"][:, :, a:b])

@@ -49,9 +49,9 @@ def tile_picked_beamcell_none_l_kernel(tc, xT, w1, w2, w3, cell, offs, out):
         nc.gpsimd.memset(warm[:], 0.0)
         nc.scalar.activation(warm_out[:], warm[:], ACT.Sigmoid)
 
+        nc.sync.dma_start(x_pair[1:P:4], pair_rows[1:P:4])
         nc.sync.dma_start(offsets[:], offs)
-        for first in (1, 3):
-            nc.sync.dma_start(x_pair[first:P:4], pair_rows[first:P:4])
+        nc.sync.dma_start(x_pair[3:P:4], pair_rows[3:P:4])
         for first, step in ((0, 4), (2, 4), (1, 2)):
             nc.sync.dma_start(x_rows[2][first:P:step], x_planes[first:P:step, 2, :])
         for first in range(2):

@@ -22,7 +22,7 @@ EIGHTH = S // 8
 LANES = 16
 EARLY = S - QUARTER
 I_SCALAR = 96
-CELL_VECTOR = S - 128
+CELL_VECTOR = S - 160
 
 
 def tile_picked_beamcell_none_l_kernel(tc, xT, w1, w2, w3, cell, offs, out):

@@ -22,7 +22,7 @@ EIGHTH = S // 8
 LANES = 16
 EARLY = S - QUARTER
 I_SCALAR = 96
-CELL_VECTOR = S - 160
+CELL_VECTOR = S - 128
 
 
 def tile_picked_beamcell_none_l_kernel(tc, xT, w1, w2, w3, cell, offs, out):
@@ -164,12 +164,13 @@ def tile_picked_beamcell_none_l_kernel(tc, xT, w1, w2, w3, cell, offs, out):
         nc.vector.tensor_tensor(runs(fresh[:, :HALF]), i_first, runs(gate_g[:, :HALF]), ALU.mult)
         nc.vector.tensor_tensor(fresh[:, HALF:EARLY], i_third[:], gate_g[:, HALF:EARLY], ALU.mult)
         make_gate("f", 0, QUARTER, runs(forget[:, :QUARTER]), 6)
-        make_gate("f", QUARTER, EARLY, runs(forget[:, QUARTER:EARLY]), 7)
+        make_gate("f", QUARTER, HALF, runs(forget[:, QUARTER:HALF]), 7)
+        make_gate("f", HALF, EARLY, runs(forget[:, HALF:EARLY]), 1)
+        make_gate("g", EARLY, S, runs(gate_g[:, EARLY:]), 2)
         acc_last = ps.tile([P, HALF], F32, name="acc_last", tag="bank0")
         product(acc_last[:, :QUARTER], "f", EARLY, S)
         product(acc_last[:, QUARTER:], "i", EARLY, S)
         nc.scalar.activation(fresh_and_forget[:, 2 * EARLY :], acc_last[:], ACT.Sigmoid)
-        make_gate("g", EARLY, S, runs(gate_g[:, EARLY:]), 5)
 
         for a, b in ((0, QUARTER), (QUARTER, CELL_VECTOR)):
             nc.vector.tensor_tensor(kept[:, a:b], cell_rows[:].indirect(picks(a, b)), forget[:, a:b], ALU.mult)

@@ -38,7 +38,7 @@ def tile_picked_beamcell_none_l_kernel(tc, xT, w1, w2, w3, cell, offs, out):
         weights = {"f": w1, "i": w2, "g": w3}
         funcs = {"f": ACT.Sigmoid, "i": ACT.Sigmoid, "g": ACT.Tanh}
         w_raw = {n: sb.tile([P, PACK, N], F32, name=f"w_raw_{n}", tag=f"w_raw_{n}", align_bytes=256) for n in names}
-        cell_rows = sb.tile([P, T], F32, name="cell_rows", align_bytes=256)
+        cell_rows = sb.tile([P, T], F32, name="cell_rows", tag="x_rows2", align_bytes=256)
 
         x_planes = xT.rearrange("(p j) t -> p j t", j=PACK)
         pair_rows = x_planes[:, 0:2, :].rearrange("p j t -> p (j t)")

@@ -66,21 +66,18 @@ def tile_picked_beamcell_none_l_kernel(tc, xT, w1, w2, w3, cell, offs, out):
         def scalar_pick(values, window, a, b):
             nc.scalar.activation(values, window.indirect(picks(a, b)), ACT.Copy)
 
-        x_bf = sb.tile([P, EARLY, PACK], BF16, name="x_bf", align_bytes=64)
+        x_bf = sb.tile([P, HALF, PACK], BF16, name="x_bf", align_bytes=64)
+        x_third = sb.tile([P, QUARTER, PACK], BF16, name="x_third", align_bytes=64)
         picked = sb.tile([P, 2, S], F32, name="picked")
         dense = sb.tile([P, PACK, HALF], BF16, name="dense")
         late_planes = dense[:, :, QUARTER:]
         scalar_pick(picked[:, 0, :], x_pair[:], 0, S)
         nc.vector.tensor_copy(picked[:, 1, :], x_pair[:, T:].indirect(offsets[:]))
-        for a, b in ((0, HALF), (HALF, EARLY)):
-            nc.scalar.copy(x_bf[:, a:b, 0:2], picked[:, :, a:b].rearrange("p j s -> p s j"))
-        nc.vector.tensor_copy(late_planes[:, 0:2, :], picked[:, :, EARLY:])
-        nc.vector.tensor_copy(x_bf[:, :, 2], x_rows[2][:].indirect(picks(0, EARLY)))
-        scalar_pick(late_planes[:, 2, :], x_rows[2][:], EARLY, S)
-
-        scalar_pick(dense[:, 3, :], x_rows[3][:], HALF, S)
-        nc.vector.tensor_copy(x_bf[:, :HALF, 3], x_rows[3][:].indirect(picks(0, HALF)))
-        nc.vector.tensor_copy(x_bf[:, HALF:, 3], dense[:, 3, :QUARTER])
+        nc.scalar.copy(x_bf[:, :, 0:2], picked[:, :, :HALF].rearrange("p j s -> p s j"))
+        nc.vector.tensor_copy(dense[:, 0:2, :], picked[:, :, HALF:])
+        for j in (2, 3):
+            scalar_pick(dense[:, j, :], x_rows[j][:], HALF, S)
+            nc.vector.tensor_copy(x_bf[:, :, j], x_rows[j][:].indirect(picks(0, HALF)))
 
         def interleave(copy, woven, planes):
             copy(woven.rearrange("p (c e) j -> p c j e", e=4), planes.rearrange("p j (c e) -> p c j e", e=4))
@@ -109,10 +106,11 @@ def tile_picked_beamcell_none_l_kernel(tc, xT, w1, w2, w3, cell, offs, out):
         codes_mid = sb.tile([P, HALF], U32, name="codes_mid", tag="w_raw_i", align_bytes=256)
         x_bf_late = sb.tile([P, QUARTER, PACK], BF16, name="x_bf_late", tag="w_raw_g", align_bytes=256)
 
+        interleave(nc.vector.tensor_copy, x_third[:], dense[:, :, :QUARTER])
         quantise(codes_first[:], x_scales[:, :QUARTER], x_bf[:, :QUARTER, :])
         quantise_w("i", 0, N)
-        for a in (QUARTER, HALF):
-            quantise(codes_mid[:, a - QUARTER : a], x_scales[:, a : a + QUARTER], x_bf[:, a : a + QUARTER, :])
+        quantise(codes_mid[:, :QUARTER], x_scales[:, QUARTER:HALF], x_bf[:, QUARTER:, :])
+        quantise(codes_mid[:, QUARTER:], x_scales[:, HALF:EARLY], x_third[:])
         quantise_w("g", 0, N)
         interleave(nc.vector.tensor_copy, x_bf_late[:], late_planes)
         for a, b in w_halves:

@@ -66,10 +66,10 @@ def tile_picked_beamcell_none_l_kernel(tc, xT, w1, w2, w3, cell, offs, out):
         def scalar_pick(values, window, a, b):
             nc.scalar.activation(values, window.indirect(picks(a, b)), ACT.Copy)
 
-        x_bf = sb.tile([P, HALF, PACK], BF16, name="x_bf", align_bytes=64)
-        x_third = sb.tile([P, QUARTER, PACK], BF16, name="x_third", align_bytes=64)
-        picked = sb.tile([P, 2, S], F32, name="picked")
-        dense = sb.tile([P, PACK, HALF], BF16, name="dense")
+        x_bf = sb.tile([P, HALF, PACK], BF16, name="x_bf", align_bytes=256)
+        x_third = sb.tile([P, QUARTER, PACK], BF16, name="x_third", align_bytes=256)
+        picked = sb.tile([P, 2, S], F32, name="picked", align_bytes=256)
+        dense = sb.tile([P, PACK, HALF], BF16, name="dense", align_bytes=256)
         late_planes = dense[:, :, QUARTER:]
         scalar_pick(picked[:, 0, :], x_pair[:], 0, S)
         nc.vector.tensor_copy(picked[:, 1, :], x_pair[:, T:].indirect(offsets[:]))
@@ -85,9 +85,9 @@ def tile_picked_beamcell_none_l_kernel(tc, xT, w1, w2, w3, cell, offs, out):
         def gpsimd_round(rounded, values):
             nc.gpsimd.tensor_scalar(rounded, values, 1.0, 0.0, ALU.mult, ALU.add)
 
-        w_bf = {n: sb.tile([P, N, PACK], BF16, name=f"w_bf_{n}", tag=f"w_bf_{n}", align_bytes=64) for n in names}
-        w_codes = {n: sb.tile([P, N], U32, name=f"w_codes_{n}", align_bytes=64) for n in names}
-        w_scales = {n: sb.tile([P, N], U8, name=f"w_scales_{n}", align_bytes=64) for n in names}
+        w_bf = {n: sb.tile([P, N, PACK], BF16, name=f"w_bf_{n}", tag=f"w_bf_{n}", align_bytes=256) for n in names}
+        w_codes = {n: sb.tile([P, N], U32, name=f"w_codes_{n}", align_bytes=256) for n in names}
+        w_scales = {n: sb.tile([P, N], U8, name=f"w_scales_{n}", align_bytes=256) for n in names}
         w_halves = [(0, N // 2), (N // 2, N)]
         interleave(nc.scalar.copy, w_bf["i"][:, :I_SCALAR, :], w_raw["i"][:, :, :I_SCALAR])
         interleave(gpsimd_round, w_bf["i"][:, I_SCALAR:, :], w_raw["i"][:, :, I_SCALAR:])
@@ -101,7 +101,7 @@ def tile_picked_beamcell_none_l_kernel(tc, xT, w1, w2, w3, cell, offs, out):
         def quantise_w(n, a, b):
             quantise(w_codes[n][:, a:b], w_scales[n][:, a:b], w_bf[n][:, a:b, :])
 
-        x_scales = sb.tile([P, S], U8, name="x_scales", align_bytes=64)
+        x_scales = sb.tile([P, S], U8, name="x_scales", align_bytes=256)
         codes_first = sb.tile([P, QUARTER], U32, name="codes_first", tag="x_rows3", align_bytes=256)
         codes_mid = sb.tile([P, HALF], U32, name="codes_mid", tag="w_raw_i", align_bytes=256)
         x_bf_late = sb.tile([P, QUARTER, PACK], BF16, name="x_bf_late", tag="w_raw_g", align_bytes=256)
@@ -115,7 +115,7 @@ def tile_picked_beamcell_none_l_kernel(tc, xT, w1, w2, w3, cell, offs, out):
         interleave(nc.vector.tensor_copy, x_bf_late[:], late_planes)
         for a, b in w_halves:
             quantise_w("f", a, b)
-        codes_last = sb.tile([P, QUARTER], U32, name="codes_last", tag="w_bf_f", align_bytes=64)
+        codes_last = sb.tile([P, QUARTER], U32, name="codes_last", tag="w_bf_f", align_bytes=256)
         quantise(codes_last[:], x_scales[:, EARLY:], x_bf_late[:])
 
         def x_codes(a, b):
@@ -145,13 +145,13 @@ def tile_picked_beamcell_none_l_kernel(tc, xT, w1, w2, w3, cell, offs, out):
             nc.scalar.activation(values, runs(acc[:]), funcs[n])
 
         i_first = w_raw["f"][:, :, : N // 2]
-        i_third = sb.tile([P, QUARTER], F32, name="i_third")
-        gate_g = sb.tile([P, S], F32, name="gate_g")
-        fresh_and_forget = sb.tile([P, EARLY + S + QUARTER], F32, name="fresh_and_forget")
+        i_third = sb.tile([P, QUARTER], F32, name="i_third", align_bytes=256)
+        gate_g = sb.tile([P, S], F32, name="gate_g", align_bytes=256)
+        fresh_and_forget = sb.tile([P, EARLY + S + QUARTER], F32, name="fresh_and_forget", align_bytes=256)
         fresh = fresh_and_forget[:, :S]
         forget = fresh_and_forget[:, EARLY : EARLY + S]
         i_last = fresh_and_forget[:, EARLY + S :]
-        kept = sb.tile([P, S], F32, name="kept")
+        kept = sb.tile([P, S], F32, name="kept", align_bytes=256)
         result = [sb.tile([P, HALF], F32, name=f"result{h}", align_bytes=256) for h in range(2)]
 
         make_gate("i", 0, QUARTER, i_first[:, 0:2, :], 0)
@@ -172,7 +172,7 @@ def tile_picked_beamcell_none_l_kernel(tc, xT, w1, w2, w3, cell, offs, out):
 
         for a, b in ((0, QUARTER), (QUARTER, CELL_VECTOR)):
             nc.vector.tensor_tensor(kept[:, a:b], cell_rows[:].indirect(picks(a, b)), forget[:, a:b], ALU.mult)
-        cell_last = sb.tile([P, S - CELL_VECTOR], F32, name="cell_last")
+        cell_last = sb.tile([P, S - CELL_VECTOR], F32, name="cell_last", align_bytes=256)
         nc.scalar.activation(cell_last[:], cell_rows[:].indirect(picks(CELL_VECTOR, S)), ACT.Copy)
         nc.vector.tensor_tensor(fresh[:, EARLY:], i_last, gate_g[:, EARLY:], ALU.mult)
         nc.vector.tensor_tensor(kept[:, CELL_VECTOR:], cell_last[:], forget[:, CELL_VECTOR:], ALU.mult)

from contextlib import ExitStack

import concourse.mybir as mybir

K, T, S, N = 512, 2048, 512, 128
FLOPS = 3 * 2 * K * N * S

F32 = mybir.dt.float32
BF16 = mybir.dt.bfloat16
U32 = mybir.dt.uint32
U16 = mybir.dt.uint16
U8 = mybir.dt.uint8
FP8X4 = mybir.dt.float8_e4m3fn_x4
ACT = mybir.ActivationFunctionType
ALU = mybir.AluOpType

P = 128
PACK = 4
HALF = S // 2
QUARTER = S // 4
EIGHTH = S // 8
LANES = 16
EARLY = S - QUARTER
I_SCALAR = 96
CELL_VECTOR = S - 128


def tile_picked_beamcell_none_l_kernel(tc, xT, w1, w2, w3, cell, offs, out):
    nc = tc.nc
    with ExitStack() as ctx:
        sb = ctx.enter_context(tc.tile_pool(name="sb", bufs=1))
        ps = ctx.enter_context(tc.psum_pool(name="ps", bufs=1))

        offsets = sb.tile([P, S // LANES], U16, name="offsets")
        x_pair = sb.tile([P, 2 * T], F32, name="x_pair", align_bytes=256)
        x_rows = {j: sb.tile([P, T], F32, name=f"x_rows{j}", tag=f"x_rows{j}", align_bytes=256) for j in (2, 3)}
        names = ("i", "g", "f")
        weights = {"f": w1, "i": w2, "g": w3}
        funcs = {"f": ACT.Sigmoid, "i": ACT.Sigmoid, "g": ACT.Tanh}
        w_raw = {n: sb.tile([P, PACK, N], F32, name=f"w_raw_{n}", tag=f"w_raw_{n}", align_bytes=256) for n in names}
        cell_rows = sb.tile([P, T], F32, name="cell_rows", tag="x_rows2", align_bytes=256)

        x_planes = xT.rearrange("(p j) t -> p j t", j=PACK)
        pair_rows = x_planes[:, 0:2, :].rearrange("p j t -> p (j t)")
        nc.scalar.dma_start(x_pair[0:P:2], pair_rows[0:P:2])

        warm = sb.tile([P, 8], F32, name="warm")
        warm_out = sb.tile([P, 8], F32, name="warm_out")
        nc.gpsimd.memset(warm[:], 0.0)
        nc.scalar.activation(warm_out[:], warm[:], ACT.Sigmoid)

        nc.sync.dma_start(x_pair[1:P:4], pair_rows[1:P:4])
        nc.sync.dma_start(offsets[:], offs)
        nc.sync.dma_start(x_pair[3:P:4], pair_rows[3:P:4])
        for first, step in ((0, 4), (2, 4), (1, 2)):
            nc.sync.dma_start(x_rows[2][first:P:step], x_planes[first:P:step, 2, :])
        for first in range(2):
            nc.sync.dma_start(x_rows[3][first:P:2], x_planes[first:P:2, 3, :])
        for n in names:
            nc.sync.dma_start(w_raw[n][:], weights[n].rearrange("(p j) m -> p j m", j=PACK))
        nc.sync.dma_start(cell_rows[:], cell)

        def picks(a, b):
            return offsets[:, a // LANES : b // LANES]

        def scalar_pick(values, window, a, b):
            nc.scalar.activation(values, window.indirect(picks(a, b)), ACT.Copy)

        x_bf = sb.tile([P, HALF, PACK], BF16, name="x_bf", align_bytes=256)
        x_third = sb.tile([P, QUARTER, PACK], BF16, name="x_third", align_bytes=256)
        picked = sb.tile([P, 2, S], F32, name="picked", align_bytes=256)
        dense = sb.tile([P, PACK, HALF], BF16, name="dense", align_bytes=256)
        late_planes = dense[:, :, QUARTER:]
        scalar_pick(picked[:, 0, :], x_pair[:], 0, S)
        nc.vector.tensor_copy(picked[:, 1, :], x_pair[:, T:].indirect(offsets[:]))
        nc.scalar.copy(x_bf[:, :, 0:2], picked[:, :, :HALF].rearrange("p j s -> p s j"))
        nc.vector.tensor_copy(dense[:, 0:2, :], picked[:, :, HALF:])
        for j in (2, 3):
            scalar_pick(dense[:, j, :], x_rows[j][:], HALF, S)
            nc.vector.tensor_copy(x_bf[:, :, j], x_rows[j][:].indirect(picks(0, HALF)))

        def interleave(copy, woven, planes):
            copy(woven.rearrange("p (c e) j -> p c j e", e=4), planes.rearrange("p j (c e) -> p c j e", e=4))

        def gpsimd_round(rounded, values):
            nc.gpsimd.tensor_scalar(rounded, values, 1.0, 0.0, ALU.mult, ALU.add)

        w_bf = {n: sb.tile([P, N, PACK], BF16, name=f"w_bf_{n}", tag=f"w_bf_{n}", align_bytes=256) for n in names}
        w_codes = {n: sb.tile([P, N], U32, name=f"w_codes_{n}", align_bytes=256) for n in names}
        w_scales = {n: sb.tile([P, N], U8, name=f"w_scales_{n}", align_bytes=256) for n in names}
        w_halves = [(0, N // 2), (N // 2, N)]
        interleave(nc.scalar.copy, w_bf["i"][:, :I_SCALAR, :], w_raw["i"][:, :, :I_SCALAR])
        interleave(gpsimd_round, w_bf["i"][:, I_SCALAR:, :], w_raw["i"][:, :, I_SCALAR:])
        interleave(nc.scalar.copy, w_bf["g"][:], w_raw["g"][:])
        for a, b in w_halves:
            interleave(nc.scalar.copy, w_bf["f"][:, a:b, :], w_raw["f"][:, :, a:b])

        def quantise(codes, scales, woven):
            nc.vector.quantize_mx(codes.bitcast(FP8X4), scales, woven.rearrange("p c j -> p (c j)"))

        def quantise_w(n, a, b):
            quantise(w_codes[n][:, a:b], w_scales[n][:, a:b], w_bf[n][:, a:b, :])

        x_scales = sb.tile([P, S], U8, name="x_scales", align_bytes=256)
        codes_first = sb.tile([P, QUARTER], U32, name="codes_first", tag="x_rows3", align_bytes=256)
        codes_mid = sb.tile([P, HALF], U32, name="codes_mid", tag="w_raw_i", align_bytes=256)
        x_bf_late = sb.tile([P, QUARTER, PACK], BF16, name="x_bf_late", tag="w_raw_g", align_bytes=256)

        interleave(nc.vector.tensor_copy, x_third[:], dense[:, :, :QUARTER])
        quantise(codes_first[:], x_scales[:, :QUARTER], x_bf[:, :QUARTER, :])
        quantise_w("i", 0, N)
        quantise(codes_mid[:, :QUARTER], x_scales[:, QUARTER:HALF], x_bf[:, QUARTER:, :])
        quantise(codes_mid[:, QUARTER:], x_scales[:, HALF:EARLY], x_third[:])
        quantise_w("g", 0, N)
        interleave(nc.vector.tensor_copy, x_bf_late[:], late_planes)
        for a, b in w_halves:
            quantise_w("f", a, b)
        codes_last = sb.tile([P, QUARTER], U32, name="codes_last", tag="w_bf_f", align_bytes=256)
        quantise(codes_last[:], x_scales[:, EARLY:], x_bf_late[:])

        def x_codes(a, b):
            if a < QUARTER:
                return codes_first[:]
            if a < EARLY:
                return codes_mid[:, a - QUARTER : b - QUARTER]
            return codes_last[:]

        def product(acc, n, a, b):
            nc.tensor.matmul_mx(
                acc,
                lhsT=w_codes[n][:].bitcast(FP8X4),
                lhsT_scale=w_scales[n][:],
                rhs=x_codes(a, b).bitcast(FP8X4),
                rhs_scale=x_scales[:, a:b],
                start=True,
                stop=True,
            )

        def runs(ap):
            return ap.rearrange("p (r c) -> p r c", c=EIGHTH)

        def make_gate(n, a, b, values, bank):
            acc = ps.tile([P, b - a], F32, name=f"acc_{n}{a}", tag=f"bank{bank}")
            product(acc[:], n, a, b)
            nc.scalar.activation(values, runs(acc[:]), funcs[n])

        i_first = w_raw["f"][:, :, : N // 2]
        i_third = sb.tile([P, QUARTER], F32, name="i_third", align_bytes=256)
        gate_g = sb.tile([P, S], F32, name="gate_g", align_bytes=256)
        fresh_and_forget = sb.tile([P, EARLY + S + QUARTER], F32, name="fresh_and_forget", align_bytes=256)
        fresh = fresh_and_forget[:, :S]
        forget = fresh_and_forget[:, EARLY : EARLY + S]
        i_last = fresh_and_forget[:, EARLY + S :]
        kept = sb.tile([P, S], F32, name="kept", align_bytes=256)
        result = [sb.tile([P, HALF], F32, name=f"result{h}", align_bytes=256) for h in range(2)]

        make_gate("i", 0, QUARTER, i_first[:, 0:2, :], 0)
        make_gate("i", QUARTER, HALF, i_first[:, 2:4, :], 1)
        make_gate("i", HALF, EARLY, runs(i_third[:]), 2)
        for u in range(3):
            make_gate("g", u * QUARTER, (u + 1) * QUARTER, runs(gate_g[:, u * QUARTER : (u + 1) * QUARTER]), 3 + u)
        nc.vector.tensor_tensor(runs(fresh[:, :HALF]), i_first, runs(gate_g[:, :HALF]), ALU.mult)
        nc.vector.tensor_tensor(fresh[:, HALF:EARLY], i_third[:], gate_g[:, HALF:EARLY], ALU.mult)
        make_gate("f", 0, QUARTER, runs(forget[:, :QUARTER]), 6)
        make_gate("f", QUARTER, HALF, runs(forget[:, QUARTER:HALF]), 7)
        make_gate("f", HALF, EARLY, runs(forget[:, HALF:EARLY]), 1)
        make_gate("g", EARLY, S, runs(gate_g[:, EARLY:]), 2)
        acc_last = ps.tile([P, HALF], F32, name="acc_last", tag="bank0")
        product(acc_last[:, :QUARTER], "f", EARLY, S)
        product(acc_last[:, QUARTER:], "i", EARLY, S)
        nc.scalar.activation(fresh_and_forget[:, 2 * EARLY :], acc_last[:], ACT.Sigmoid)

        for a, b in ((0, QUARTER), (QUARTER, CELL_VECTOR)):
            nc.vector.tensor_tensor(kept[:, a:b], cell_rows[:].indirect(picks(a, b)), forget[:, a:b], ALU.mult)
        cell_last = sb.tile([P, S - CELL_VECTOR], F32, name="cell_last", align_bytes=256)
        nc.scalar.activation(cell_last[:], cell_rows[:].indirect(picks(CELL_VECTOR, S)), ACT.Copy)
        nc.vector.tensor_tensor(fresh[:, EARLY:], i_last, gate_g[:, EARLY:], ALU.mult)
        nc.vector.tensor_tensor(kept[:, CELL_VECTOR:], cell_last[:], forget[:, CELL_VECTOR:], ALU.mult)
        for h in range(2):
            cols = slice(h * HALF, (h + 1) * HALF)
            nc.vector.tensor_tensor(result[h][:], kept[:, cols], fresh[:, cols], ALU.add)
            nc.sync.dma_start(out[:, cols], result[h][:])
